import numpy as np
import ml_dtypes


def mxq(x, axis, fmt="e4m3"):
    dtype, down = {"e4m3": (ml_dtypes.float8_e4m3fn, 7), "e5m2": (ml_dtypes.float8_e5m2, 14)}[fmt]
    v = np.moveaxis(np.asarray(x, np.float32).astype(ml_dtypes.bfloat16).astype(np.float64), axis, -1)
    blocks = v.reshape(v.shape[:-1] + (-1, 32))
    amax = np.abs(blocks).max(-1, keepdims=True)
    byte = np.maximum(np.where(amax > 0, np.frexp(amax)[1] - 1 + 127, 0) - down, 1)
    scale = np.exp2(byte - 127.0)
    codes = (blocks / scale).astype(np.float32).astype(dtype).astype(np.float64)
    return np.moveaxis((codes * scale).reshape(v.shape), -1, axis)


WIDE = False


def mx_kscale(k):
    if not WIDE:
        return np.ones(k)
    levels = np.array([10, -10, 5, -5, 0])
    if k % 512:
        return np.exp2(np.random.permutation(np.resize(levels, k // 32))).repeat(32)
    a = np.empty((k // 512, 16))
    for p in range(k // 512):
        a[p, :8] = np.random.permutation(np.resize(levels, 8))
        for g in range(8):
            far = levels[np.abs(levels - a[p, g]) >= 10]
            a[p, g + 8] = far[np.random.randint(len(far))]
    return np.exp2(a.ravel()).repeat(32)


def f64(x):
    return np.asarray(x).astype(np.float64)


def striped(idx):
    return np.tile(idx.reshape(-1, 16).T, (8, 1)).astype(np.uint16)


def unstriped(offs):
    return offs[:16].T.reshape(-1).astype(np.int64)


def pack_weight(w):
    k, n = w.shape
    w = f64(np.asarray(w, np.float32).astype(ml_dtypes.bfloat16)).reshape(k // 32, 32, n)
    amax = np.abs(w).max(1)
    byte = np.clip(np.where(amax > 0, np.frexp(amax)[1] - 1 + 127 - 7, 1), 1, 254)
    scaled = (w * np.exp2(127.0 - byte)[:, None, :]).reshape(k, n).astype(np.float32)
    words = np.ascontiguousarray(scaled.reshape(k // 512, 128, 4, n).transpose(0, 1, 3, 2)).astype(ml_dtypes.float8_e4m3fn).view(np.uint8)
    return words, np.ascontiguousarray(byte.astype(np.uint8).reshape(k // 512, 16, n))


def unpack_weight(words, scales):
    g, p, n, _ = words.shape
    vals = np.ascontiguousarray(words).view(ml_dtypes.float8_e4m3fn).astype(np.float64) * np.repeat(np.exp2(scales.astype(np.float64) - 127.0), 8, axis=1)[..., None]
    return vals.transpose(0, 1, 3, 2).reshape(g * 512, n)


K, T, S, V, N, U = 512, 1024, 512, 256, 256, 512


def setup_inputs():
    n = np.random.standard_normal
    s = mx_kscale(K)[:, None]
    packed_w1 = pack_weight(n((K, N)) / np.sqrt(2 * K) / s)
    packed_w2 = pack_weight(n((K, N)) / np.sqrt(2 * K) / s)
    return {
        "xT": (n((K, T)) * s).astype(np.float32),
        "w1_words": packed_w1[0],
        "w1_scales": packed_w1[1],
        "w2_words": packed_w2[0],
        "w2_scales": packed_w2[1],
        "offs": striped(np.random.permutation(T)[:S]),
        "to1": striped(np.random.permutation(U)[:V]),
        "to2": striped(np.random.permutation(U)[:V]),
    }


def reference(xT, w1_words, w1_scales, w2_words, w2_scales, offs, to1, to2):
    xq = mxq(f64(xT)[:, unstriped(offs)], 0, "e4m3")
    o0 = np.zeros((N, S))
    o0[:, unstriped(to1)] = unpack_weight(w1_words, w1_scales).T @ xq[:, :V]
    o1 = np.zeros((N, S))
    o1[:, unstriped(to2)] = unpack_weight(w2_words, w2_scales).T @ xq[:, V:2 * V]
    return o0 + o1

@@ -1,0 +1,154 @@
+from contextlib import ExitStack
+
+import concourse.mybir as mybir
+
+K, T, V, N, U = 512, 1024, 256, 256, 512
+FLOPS = 2 * 2 * K * V * N
+
+F32 = mybir.dt.float32
+BF16 = mybir.dt.bfloat16
+I32 = mybir.dt.int32
+U32 = mybir.dt.uint32
+U16 = mybir.dt.uint16
+U8 = mybir.dt.uint8
+FP8X4 = mybir.dt.float8_e4m3fn_x4
+ADD = mybir.AluOpType.add
+
+P = 128
+PACK = 4
+TAPS = 2
+BLOCKS = N // P
+PIECES = ((0, 0, 128), (0, 128, 128), (1, 0, 256))
+
+
+def tile_picked_spconv_none_e_kernel(tc, xT, w1_words, w1_scales, w2_words, w2_scales, offs, to1, to2, out):
+    nc = tc.nc
+    with ExitStack() as ctx:
+        keep = ctx.enter_context(tc.tile_pool(name="keep", bufs=1))
+        psum = ctx.enter_context(tc.psum_pool(name="psum", bufs=1))
+
+        offs_sb = keep.tile([P, TAPS * V // 16], U16, name="offs_sb")
+        to_sb = [keep.tile([P, V // 16], U16, name="to%d" % d) for d in range(TAPS)]
+        planes = [keep.tile([P, T], F32, name="plane%d" % j) for j in range(PACK)]
+        w_words = [keep.tile([P, N], U32, name="w_words%d" % d, align_bytes=64) for d in range(TAPS)]
+        w_scales = [keep.tile([P, N], U8, name="w_scales%d" % d, align_bytes=64) for d in range(TAPS)]
+        x_rows = xT.rearrange("(p j) t -> j p t", j=PACK)
+
+        def load_scales(d, scales):
+            for q in range(4):
+                rows = scales[0, 4 * q : 4 * q + 4, :].bitcast(I32)
+                nc.sync.dma_start(
+                    out=w_scales[d][32 * q : 32 * q + 32, :].bitcast(I32),
+                    in_=rows.unsqueeze(0).broadcast_to([8, 4, N // 4]),
+                )
+
+        def load_words(d, words):
+            nc.sync.dma_start(out=w_words[d][:].bitcast(I32), in_=words[0].rearrange("p n t -> p (n t)").bitcast(I32))
+
+        nc.sync.dma_start(out=planes[0][:], in_=x_rows[0])
+        nc.sync.dma_start(offs_sb[:], offs)
+        for j in range(1, PACK):
+            nc.sync.dma_start(out=planes[j][:], in_=x_rows[j])
+        load_words(0, w1_words)
+        load_scales(0, w1_scales)
+        nc.sync.dma_start(to_sb[0][:], to1)
+        load_words(1, w2_words)
+        load_scales(1, w2_scales)
+        nc.sync.dma_start(to_sb[1][:], to2)
+
+        windows = [[keep.tile([P, U], F32, name="window%d_%d" % (d, b)) for b in range(BLOCKS)] for d in range(TAPS)]
+        for d in range(TAPS):
+            for b in range(BLOCKS):
+                nc.vector.memset(windows[d][b][:], 0.0)
+
+        stage = keep.tile([P, PACK * TAPS * V + 128], F32, name="stage", align_bytes=64)
+        picked = stage[:, 0 : PACK * TAPS * V].rearrange("p (j v) -> p j v", j=PACK)
+        for j in range(PACK - 1):
+            nc.vector.tensor_copy(picked[:, j, :], planes[j][:].indirect(offs_sb[:]))
+
+        def gather_last(e0, n):
+            nc.vector.tensor_copy(
+                picked[:, PACK - 1, e0 : e0 + n],
+                planes[PACK - 1][:].indirect(offs_sb[:, e0 // 16 : (e0 + n) // 16]),
+            )
+
+        for e0 in (0, 128, 256):
+            gather_last(e0, 128)
+
+        codes, scales, results = {}, {}, {}
+
+        def weave(i, tag):
+            d, v0, n = PIECES[i]
+            e0 = d * V + v0
+            if tag is None:
+                woven = stage[:, 1920:2176].bitcast(BF16).rearrange("p (v j) -> p v j", j=PACK)
+            else:
+                woven = keep.tile([P, n, PACK], BF16, name="woven%d" % i, tag=tag, align_bytes=64)[:]
+            nc.scalar.copy(out=woven, in_=picked[:, :, e0 : e0 + n].rearrange("p j v -> p v j"))
+            return woven
+
+        def quantize(i, woven):
+            n = PIECES[i][2]
+            codes[i] = keep.tile([P, n], U32, name="codes%d" % i, tag="codes%d" % i, align_bytes=64)
+            scales[i] = keep.tile([P, n], U8, name="scales%d" % i, align_bytes=64)
+            nc.vector.quantize_mx(
+                out=codes[i][:].bitcast(FP8X4), scales=scales[i][:], in_=woven.rearrange("p v j -> p (v j)")
+            )
+
+        def product(i):
+            d, v0, n = PIECES[i]
+            accs = []
+            for b in range(BLOCKS):
+                acc = psum.tile([P, 512], F32, name="acc%d_%d" % (i, b))
+                m = slice(b * P, (b + 1) * P)
+                nc.tensor.matmul_mx(
+                    out=acc[:, 0:n],
+                    lhsT=w_words[d][:, m].bitcast(FP8X4),
+                    lhsT_scale=w_scales[d][:, m],
+                    rhs=codes[i][:].bitcast(FP8X4),
+                    rhs_scale=scales[i][:],
+                    start=True,
+                    stop=True,
+                )
+                accs.append(acc)
+            return accs
+
+        def drain(i, accs):
+            n = PIECES[i][2]
+            for b in range(BLOCKS):
+                y = keep.tile([P, n], F32, name="y%d_%d" % (i, b))
+                nc.scalar.copy(out=y[:], in_=accs[b][:, 0:n])
+                results[i, b] = y
+
+        def scatter(i):
+            d, v0, n = PIECES[i]
+            for b in range(BLOCKS):
+                nc.vector.tensor_copy(
+                    windows[d][b][:].indirect(to_sb[d][:, v0 // 16 : (v0 + n) // 16]), results[i, b][:]
+                )
+
+        woven0 = weave(0, None)
+        woven1 = weave(1, "woven1")
+        quantize(0, woven0)
+        gather_last(384, 128)
+        quantize(1, woven1)
+        accs0 = product(0)
+        accs1 = product(1)
+        drain(0, accs0)
+        woven2 = weave(2, "codes0")
+        scatter(0)
+        quantize(2, woven2)
+        drain(1, accs1)
+        accs2 = product(2)
+        scatter(1)
+        drain(2, accs2)
+        scatter(2)
+
+        total0 = keep.tile([P, U], F32, name="total0")
+        nc.gpsimd.tensor_tensor(total0[:], windows[0][0][:], windows[1][0][:], ADD)
+        nc.sync.dma_start(out=out[0:P, :], in_=total0[:])
+        for h, queue in enumerate((nc.sync, nc.scalar)):
+            cols = slice(h * (U // 2), (h + 1) * (U // 2))
+            half = keep.tile([P, U // 2], F32, name="half%d" % h)
+            nc.vector.tensor_tensor(half[:], windows[0][1][:, cols], windows[1][1][:, cols], ADD)
+            queue.dma_start(out=out[P : 2 * P, cols], in_=half[:])

@@ -1,6 +1,7 @@
 from contextlib import ExitStack
 
 import concourse.mybir as mybir
+from concourse.masks import make_identity
 
 K, T, V, N, U = 512, 1024, 256, 256, 512
 FLOPS = 2 * 2 * K * V * N
@@ -18,7 +19,7 @@ P = 128
 PACK = 4
 TAPS = 2
 BLOCKS = N // P
-PIECES = ((0, 0, 128), (0, 128, 128), (1, 0, 256))
+PIECES = ((1, 0, 128), (0, 0, 256), (1, 128, 128))
 
 
 def tile_picked_spconv_none_e_kernel(tc, xT, w1_words, w1_scales, w2_words, w2_scales, offs, to1, to2, out):
@@ -49,18 +50,20 @@ def tile_picked_spconv_none_e_kernel(tc, xT, w1_words, w1_scales, w2_words, w2_s
         nc.sync.dma_start(offs_sb[:], offs)
         for j in range(1, PACK):
             nc.sync.dma_start(out=planes[j][:], in_=x_rows[j])
-        load_words(0, w1_words)
-        load_scales(0, w1_scales)
-        nc.sync.dma_start(to_sb[0][:], to1)
         load_words(1, w2_words)
         load_scales(1, w2_scales)
         nc.sync.dma_start(to_sb[1][:], to2)
+        nc.sync.dma_start(to_sb[0][:], to1)
+        load_words(0, w1_words)
+        load_scales(0, w1_scales)
 
         windows = [[keep.tile([P, U], F32, name="window%d_%d" % (d, b)) for b in range(BLOCKS)] for d in range(TAPS)]
         for d in range(TAPS):
             for b in range(BLOCKS):
                 nc.vector.memset(windows[d][b][:], 0.0)
 
+        ident = keep.tile([P, P], F32, name="ident")
+        make_identity(nc, ident[:])
         stage = keep.tile([P, PACK * TAPS * V + 128], F32, name="stage", align_bytes=64)
         picked = stage[:, 0 : PACK * TAPS * V].rearrange("p (j v) -> p j v", j=PACK)
         for j in range(PACK - 1):
@@ -72,34 +75,34 @@ def tile_picked_spconv_none_e_kernel(tc, xT, w1_words, w1_scales, w2_words, w2_s
                 planes[PACK - 1][:].indirect(offs_sb[:, e0 // 16 : (e0 + n) // 16]),
             )
 
-        for e0 in (0, 128, 256):
+        for e0 in (256, 0, 128):
             gather_last(e0, 128)
 
         codes, scales, results = {}, {}, {}
 
-        def weave(i, tag):
-            d, v0, n = PIECES[i]
-            e0 = d * V + v0
-            if tag is None:
-                woven = stage[:, 1920:2176].bitcast(BF16).rearrange("p (v j) -> p v j", j=PACK)
-            else:
-                woven = keep.tile([P, n, PACK], BF16, name="woven%d" % i, tag=tag, align_bytes=64)[:]
-            nc.scalar.copy(out=woven, in_=picked[:, :, e0 : e0 + n].rearrange("p j v -> p v j"))
-            return woven
+        def weave(woven, e0):
+            nc.scalar.copy(out=woven, in_=picked[:, :, e0 : e0 + 128].rearrange("p j v -> p v j"))
 
-        def quantize(i, woven):
+        def woven_tile(name, tag):
+            return keep.tile([P, 128, PACK], BF16, name=name, tag=tag, align_bytes=64)[:]
+
+        def operand(i):
             n = PIECES[i][2]
             codes[i] = keep.tile([P, n], U32, name="codes%d" % i, tag="codes%d" % i, align_bytes=64)
-            scales[i] = keep.tile([P, n], U8, name="scales%d" % i, align_bytes=64)
+            scales[i] = keep.tile([P, n], U8, name="scales%d" % i, tag="scales%d" % min(i, 1), align_bytes=64)
+
+        def quantize(i, v0, woven):
             nc.vector.quantize_mx(
-                out=codes[i][:].bitcast(FP8X4), scales=scales[i][:], in_=woven.rearrange("p v j -> p (v j)")
+                out=codes[i][:, v0 : v0 + 128].bitcast(FP8X4),
+                scales=scales[i][:, v0 : v0 + 128],
+                in_=woven.rearrange("p v j -> p (v j)"),
             )
 
         def product(i):
             d, v0, n = PIECES[i]
             accs = []
             for b in range(BLOCKS):
-                acc = psum.tile([P, 512], F32, name="acc%d_%d" % (i, b))
+                acc = psum.tile([P, 512], F32, name="acc%d_%d" % (i, b), tag="acc%d_%d" % (i, b))
                 m = slice(b * P, (b + 1) * P)
                 nc.tensor.matmul_mx(
                     out=acc[:, 0:n],
@@ -113,42 +116,79 @@ def tile_picked_spconv_none_e_kernel(tc, xT, w1_words, w1_scales, w2_words, w2_s
                 accs.append(acc)
             return accs
 
-        def drain(i, accs):
+        def drain(i, b, accs, tag):
             n = PIECES[i][2]
-            for b in range(BLOCKS):
-                y = keep.tile([P, n], F32, name="y%d_%d" % (i, b))
-                nc.scalar.copy(out=y[:], in_=accs[b][:, 0:n])
-                results[i, b] = y
+            y = keep.tile([P, n], F32, name="y%d_%d" % (i, b), tag=tag, align_bytes=64)
+            nc.scalar.copy(out=y[:], in_=accs[b][:, 0:n])
+            results[i, b] = y
 
-        def scatter(i):
+        def scatter(i, b):
             d, v0, n = PIECES[i]
-            for b in range(BLOCKS):
-                nc.vector.tensor_copy(
-                    windows[d][b][:].indirect(to_sb[d][:, v0 // 16 : (v0 + n) // 16]), results[i, b][:]
-                )
+            nc.vector.tensor_copy(
+                windows[d][b][:].indirect(to_sb[d][:, v0 // 16 : (v0 + n) // 16]), results[i, b][:]
+            )
 
-        woven0 = weave(0, None)
-        woven1 = weave(1, "woven1")
-        quantize(0, woven0)
+        woven0 = stage[:, 1920:2176].bitcast(BF16).rearrange("p (v j) -> p v j", j=PACK)
+        weave(woven0, 256)
+        woven1a = woven_tile("woven1a", "woven1a")
+        weave(woven1a, 0)
+        operand(0)
+        quantize(0, 0, woven0)
         gather_last(384, 128)
-        quantize(1, woven1)
+        operand(1)
+        quantize(1, 0, woven1a)
         accs0 = product(0)
+        drain(0, 0, accs0, "y0_0")
+        woven1b = woven_tile("woven1b", "codes0")
+        weave(woven1b, 128)
+        drain(0, 1, accs0, "y0_1")
+        woven2 = woven_tile("woven2", "scales0")
+        weave(woven2, 384)
+        scatter(0, 0)
+        quantize(1, 128, woven1b)
         accs1 = product(1)
-        drain(0, accs0)
-        woven2 = weave(2, "codes0")
-        scatter(0)
-        quantize(2, woven2)
-        drain(1, accs1)
+        scatter(0, 1)
+        operand(2)
+        quantize(2, 0, woven2)
+        drain(1, 0, accs1, "y1_0")
         accs2 = product(2)
-        scatter(1)
-        drain(2, accs2)
-        scatter(2)
+        scatter(1, 0)
+        drain(2, 0, accs2, "y2_0")
+        drain(2, 1, accs2, "y2_1")
+        drain(1, 1, accs1, "codes2")
+        scatter(2, 0)
+        scatter(2, 1)
+        scatter(1, 1)
 
-        total0 = keep.tile([P, U], F32, name="total0")
-        nc.gpsimd.tensor_tensor(total0[:], windows[0][0][:], windows[1][0][:], ADD)
-        nc.sync.dma_start(out=out[0:P, :], in_=total0[:])
-        for h, queue in enumerate((nc.sync, nc.scalar)):
+        turned = []
+        for c, tag in enumerate(("acc2_0", "acc2_1", "acc1_1", "turn3")):
+            turned.append(psum.tile([P, 512], F32, name="turn%d" % c, tag=tag))
+
+        def turn(c, d, start):
+            nc.tensor.matmul(
+                turned[c][:, 0:P], windows[d][0][:, c * P : (c + 1) * P], ident[:],
+                start=start, stop=not start, is_transpose=True,
+            )
+
+        for c in range(3):
+            turn(c, 0, True)
+        for c in range(3):
+            turn(c, 1, False)
+        turn(3, 1, True)
+        turn(3, 0, False)
+        summed = []
+        for c in range(4):
+            summed.append(keep.tile([P, P], F32, name="summed%d" % c))
+            nc.scalar.copy(out=summed[c][:], in_=turned[c][:, 0:P])
+        for h, tag in enumerate(("acc0_0", "acc0_1")):
+            back = psum.tile([P, 512], F32, name="back%d" % h, tag=tag)
+            for c in range(2):
+                nc.tensor.transpose(back[:, c * P : (c + 1) * P], summed[2 * h + c][:], ident[:])
+            first = keep.tile([P, U // 2], F32, name="first%d" % h)
+            nc.scalar.copy(out=first[:], in_=back[:, 0 : U // 2])
+            nc.scalar.dma_start(out=out[0:P, h * (U // 2) : (h + 1) * (U // 2)], in_=first[:])
+        for h in range(2):
             cols = slice(h * (U // 2), (h + 1) * (U // 2))
             half = keep.tile([P, U // 2], F32, name="half%d" % h)
             nc.vector.tensor_tensor(half[:], windows[0][1][:, cols], windows[1][1][:, cols], ADD)
-            queue.dma_start(out=out[P : 2 * P, cols], in_=half[:])
+            nc.sync.dma_start(out=out[P : 2 * P, cols], in_=half[:])

@@ -19,7 +19,7 @@ P = 128
 PACK = 4
 TAPS = 2
 BLOCKS = N // P
-PIECES = ((1, 0, 128), (0, 0, 256), (1, 128, 128))
+PIECES = ((1, 128, 128), (0, 0, 256), (1, 0, 128))
 
 
 def tile_picked_spconv_none_e_kernel(tc, xT, w1_words, w1_scales, w2_words, w2_scales, offs, to1, to2, out):
@@ -64,38 +64,24 @@ def tile_picked_spconv_none_e_kernel(tc, xT, w1_words, w1_scales, w2_words, w2_s
 
         ident = keep.tile([P, P], F32, name="ident")
         make_identity(nc, ident[:])
-        stage = keep.tile([P, PACK * TAPS * V + 128], F32, name="stage", align_bytes=64)
-        picked = stage[:, 0 : PACK * TAPS * V].rearrange("p (j v) -> p j v", j=PACK)
+        picked = keep.tile([P, PACK, TAPS * V], F32, name="picked")
         for j in range(PACK - 1):
             nc.vector.tensor_copy(picked[:, j, :], planes[j][:].indirect(offs_sb[:]))
 
-        def gather_last(e0, n):
-            nc.vector.tensor_copy(
-                picked[:, PACK - 1, e0 : e0 + n],
-                planes[PACK - 1][:].indirect(offs_sb[:, e0 // 16 : (e0 + n) // 16]),
-            )
+        def gather_last(target, e0, n):
+            nc.vector.tensor_copy(target, planes[PACK - 1][:].indirect(offs_sb[:, e0 // 16 : (e0 + n) // 16]))
 
-        for e0 in (256, 0, 128):
-            gather_last(e0, 128)
+        def weave(woven, j, pair):
+            nc.scalar.copy(out=woven[:, :, j : j + 2], in_=pair.rearrange("p j v -> p v j"))
 
         codes, scales, results = {}, {}, {}
 
-        def weave(woven, e0):
-            nc.scalar.copy(out=woven, in_=picked[:, :, e0 : e0 + 128].rearrange("p j v -> p v j"))
-
-        def woven_tile(name, tag):
-            return keep.tile([P, 128, PACK], BF16, name=name, tag=tag, align_bytes=64)[:]
-
-        def operand(i):
+        def quantize(i, woven):
             n = PIECES[i][2]
             codes[i] = keep.tile([P, n], U32, name="codes%d" % i, tag="codes%d" % i, align_bytes=64)
             scales[i] = keep.tile([P, n], U8, name="scales%d" % i, tag="scales%d" % min(i, 1), align_bytes=64)
-
-        def quantize(i, v0, woven):
             nc.vector.quantize_mx(
-                out=codes[i][:, v0 : v0 + 128].bitcast(FP8X4),
-                scales=scales[i][:, v0 : v0 + 128],
-                in_=woven.rearrange("p v j -> p (v j)"),
+                out=codes[i][:].bitcast(FP8X4), scales=scales[i][:], in_=woven[:].rearrange("p v j -> p (v j)")
             )
 
         def product(i):
@@ -128,28 +114,27 @@ def tile_picked_spconv_none_e_kernel(tc, xT, w1_words, w1_scales, w2_words, w2_s
                 windows[d][b][:].indirect(to_sb[d][:, v0 // 16 : (v0 + n) // 16]), results[i, b][:]
             )
 
-        woven0 = stage[:, 1920:2176].bitcast(BF16).rearrange("p (v j) -> p v j", j=PACK)
-        weave(woven0, 256)
-        woven1a = woven_tile("woven1a", "woven1a")
-        weave(woven1a, 0)
-        operand(0)
-        quantize(0, 0, woven0)
-        gather_last(384, 128)
-        operand(1)
-        quantize(1, 0, woven1a)
+        woven0 = keep.tile([P, 128, PACK], BF16, name="woven0", align_bytes=64)
+        woven1 = keep.tile([P, 256, PACK], BF16, name="woven1", align_bytes=64)
+        weave(woven0, 0, picked[:, 0:2, 384:512])
+        weave(woven1, 0, picked[:, 0:2, 0:256])
+        gather_last(picked[:, 3, 384:512], 384, 128)
+        gather_last(picked[:, 3, 0:256], 0, 256)
+        weave(woven0, 2, picked[:, 2:4, 384:512])
+        weave(woven1, 2, picked[:, 2:4, 0:256])
+        quantize(0, woven0)
+        gather_last(picked[:, 2, 384:512], 256, 128)
+        quantize(1, woven1)
         accs0 = product(0)
-        drain(0, 0, accs0, "y0_0")
-        woven1b = woven_tile("woven1b", "codes0")
-        weave(woven1b, 128)
-        drain(0, 1, accs0, "y0_1")
-        woven2 = woven_tile("woven2", "scales0")
-        weave(woven2, 384)
-        scatter(0, 0)
-        quantize(1, 128, woven1b)
         accs1 = product(1)
+        drain(0, 0, accs0, "y0_0")
+        drain(0, 1, accs0, "y0_1")
+        woven2 = keep.tile([P, 128, PACK], BF16, name="woven2", tag="scales0", align_bytes=64)
+        weave(woven2, 0, picked[:, 0:2, 256:384])
+        weave(woven2, 2, picked[:, 2, 256:512].rearrange("p (j v) -> p j v", j=2))
+        scatter(0, 0)
         scatter(0, 1)
-        operand(2)
-        quantize(2, 0, woven2)
+        quantize(2, woven2)
         drain(1, 0, accs1, "y1_0")
         accs2 = product(2)
         scatter(1, 0)
@@ -161,7 +146,7 @@ def tile_picked_spconv_none_e_kernel(tc, xT, w1_words, w1_scales, w2_words, w2_s
         scatter(1, 1)
 
         turned = []
-        for c, tag in enumerate(("acc2_0", "acc2_1", "acc1_1", "turn3")):
+        for c, tag in enumerate(("turn0", "turn1", "acc2_0", "acc1_0")):
             turned.append(psum.tile([P, 512], F32, name="turn%d" % c, tag=tag))
 
         def turn(c, d, start):
@@ -170,12 +155,10 @@ def tile_picked_spconv_none_e_kernel(tc, xT, w1_words, w1_scales, w2_words, w2_s
                 start=start, stop=not start, is_transpose=True,
             )
 
-        for c in range(3):
+        for c in range(4):
             turn(c, 0, True)
-        for c in range(3):
+        for c in range(4):
             turn(c, 1, False)
-        turn(3, 1, True)
-        turn(3, 0, False)
         summed = []
         for c in range(4):
             summed.append(keep.tile([P, P], F32, name="summed%d" % c))

@@ -19,7 +19,7 @@ P = 128
 PACK = 4
 TAPS = 2
 BLOCKS = N // P
-PIECES = ((1, 128, 128), (0, 0, 256), (1, 0, 128))
+PIECES = ((1, 0, 128), (0, 0, 256), (1, 128, 128))
 
 
 def tile_picked_spconv_none_e_kernel(tc, xT, w1_words, w1_scales, w2_words, w2_scales, offs, to1, to2, out):
@@ -44,7 +44,11 @@ def tile_picked_spconv_none_e_kernel(tc, xT, w1_words, w1_scales, w2_words, w2_s
                 )
 
         def load_words(d, words):
-            nc.sync.dma_start(out=w_words[d][:].bitcast(I32), in_=words[0].rearrange("p n t -> p (n t)").bitcast(I32))
+            for b in range(BLOCKS):
+                m = slice(b * P, (b + 1) * P)
+                nc.sync.dma_start(
+                    out=w_words[d][:, m].bitcast(I32), in_=words[0, :, m, :].rearrange("p n t -> p (n t)").bitcast(I32)
+                )
 
         nc.sync.dma_start(out=planes[0][:], in_=x_rows[0])
         nc.sync.dma_start(offs_sb[:], offs)
@@ -53,8 +57,8 @@ def tile_picked_spconv_none_e_kernel(tc, xT, w1_words, w1_scales, w2_words, w2_s
         load_words(1, w2_words)
         load_scales(1, w2_scales)
         nc.sync.dma_start(to_sb[1][:], to2)
-        nc.sync.dma_start(to_sb[0][:], to1)
         load_words(0, w1_words)
+        nc.sync.dma_start(to_sb[0][:], to1)
         load_scales(0, w1_scales)
 
         windows = [[keep.tile([P, U], F32, name="window%d_%d" % (d, b)) for b in range(BLOCKS)] for d in range(TAPS)]
@@ -65,11 +69,13 @@ def tile_picked_spconv_none_e_kernel(tc, xT, w1_words, w1_scales, w2_words, w2_s
         ident = keep.tile([P, P], F32, name="ident")
         make_identity(nc, ident[:])
         picked = keep.tile([P, PACK, TAPS * V], F32, name="picked")
-        for j in range(PACK - 1):
-            nc.vector.tensor_copy(picked[:, j, :], planes[j][:].indirect(offs_sb[:]))
 
-        def gather_last(target, e0, n):
-            nc.vector.tensor_copy(target, planes[PACK - 1][:].indirect(offs_sb[:, e0 // 16 : (e0 + n) // 16]))
+        def gather(target, j, e0, n):
+            nc.vector.tensor_copy(target, planes[j][:].indirect(offs_sb[:, e0 // 16 : (e0 + n) // 16]))
+
+        gather(picked[:, 0, :], 0, 0, 512)
+        gather(picked[:, 1, :], 1, 0, 512)
+        gather(picked[:, 2, 0:384], 2, 0, 384)
 
         def weave(woven, j, pair):
             nc.scalar.copy(out=woven[:, :, j : j + 2], in_=pair.rearrange("p j v -> p v j"))
@@ -116,22 +122,23 @@ def tile_picked_spconv_none_e_kernel(tc, xT, w1_words, w1_scales, w2_words, w2_s
 
         woven0 = keep.tile([P, 128, PACK], BF16, name="woven0", align_bytes=64)
         woven1 = keep.tile([P, 256, PACK], BF16, name="woven1", align_bytes=64)
-        weave(woven0, 0, picked[:, 0:2, 384:512])
+        weave(woven0, 0, picked[:, 0:2, 256:384])
         weave(woven1, 0, picked[:, 0:2, 0:256])
-        gather_last(picked[:, 3, 384:512], 384, 128)
-        gather_last(picked[:, 3, 0:256], 0, 256)
-        weave(woven0, 2, picked[:, 2:4, 384:512])
+        gather(picked[:, 3, 256:384], 3, 256, 128)
+        gather(picked[:, 3, 0:256], 3, 0, 256)
+        weave(woven0, 2, picked[:, 2:4, 256:384])
         weave(woven1, 2, picked[:, 2:4, 0:256])
         quantize(0, woven0)
-        gather_last(picked[:, 2, 384:512], 256, 128)
+        gather(picked[:, 2, 256:384], 2, 384, 128)
+        gather(picked[:, 3, 256:384], 3, 384, 128)
         quantize(1, woven1)
         accs0 = product(0)
         accs1 = product(1)
         drain(0, 0, accs0, "y0_0")
         drain(0, 1, accs0, "y0_1")
         woven2 = keep.tile([P, 128, PACK], BF16, name="woven2", tag="scales0", align_bytes=64)
-        weave(woven2, 0, picked[:, 0:2, 256:384])
-        weave(woven2, 2, picked[:, 2, 256:512].rearrange("p (j v) -> p j v", j=2))
+        weave(woven2, 0, picked[:, 0:2, 384:512])
+        weave(woven2, 2, picked[:, 2:4, 256:384])
         scatter(0, 0)
         scatter(0, 1)
         quantize(2, woven2)

@@ -19,7 +19,7 @@ P = 128
 PACK = 4
 TAPS = 2
 BLOCKS = N // P
-PIECES = ((1, 0, 128), (0, 0, 256), (1, 128, 128))
+PIECES = ((0, 128, 128), (1, 0, 256), (0, 0, 128))
 
 
 def tile_picked_spconv_none_e_kernel(tc, xT, w1_words, w1_scales, w2_words, w2_scales, offs, to1, to2, out):
@@ -54,12 +54,12 @@ def tile_picked_spconv_none_e_kernel(tc, xT, w1_words, w1_scales, w2_words, w2_s
         nc.sync.dma_start(offs_sb[:], offs)
         for j in range(1, PACK):
             nc.sync.dma_start(out=planes[j][:], in_=x_rows[j])
-        load_words(1, w2_words)
-        load_scales(1, w2_scales)
-        nc.sync.dma_start(to_sb[1][:], to2)
         load_words(0, w1_words)
-        nc.sync.dma_start(to_sb[0][:], to1)
         load_scales(0, w1_scales)
+        nc.sync.dma_start(to_sb[0][:], to1)
+        load_words(1, w2_words)
+        nc.sync.dma_start(to_sb[1][:], to2)
+        load_scales(1, w2_scales)
 
         windows = [[keep.tile([P, U], F32, name="window%d_%d" % (d, b)) for b in range(BLOCKS)] for d in range(TAPS)]
         for d in range(TAPS):
@@ -68,17 +68,21 @@ def tile_picked_spconv_none_e_kernel(tc, xT, w1_words, w1_scales, w2_words, w2_s
 
         ident = keep.tile([P, P], F32, name="ident")
         make_identity(nc, ident[:])
-        picked = keep.tile([P, PACK, TAPS * V], F32, name="picked")
+        pairs = keep.tile([P, 4, 2, 128, 2], BF16, name="pairs")
+        chunks = pairs[:].rearrange("p q u v e -> p (q u v e)").bitcast(U32).rearrange("p (c v) -> p c v", v=128)
 
-        def gather(target, j, e0, n):
-            nc.vector.tensor_copy(target, planes[j][:].indirect(offs_sb[:, e0 // 16 : (e0 + n) // 16]))
+        def gather(j, e0, n, q0):
+            nc.vector.tensor_copy(
+                pairs[:, q0 : q0 + n // 128, j // 2, :, j % 2],
+                planes[j][:].indirect(offs_sb[:, e0 // 16 : (e0 + n) // 16]),
+            )
 
-        gather(picked[:, 0, :], 0, 0, 512)
-        gather(picked[:, 1, :], 1, 0, 512)
-        gather(picked[:, 2, 0:384], 2, 0, 384)
+        gather(0, 0, 512, 0)
+        gather(1, 0, 512, 0)
+        gather(2, 128, 384, 1)
 
-        def weave(woven, j, pair):
-            nc.scalar.copy(out=woven[:, :, j : j + 2], in_=pair.rearrange("p j v -> p v j"))
+        def weave(woven, words):
+            nc.scalar.copy(out=woven, in_=words)
 
         codes, scales, results = {}, {}, {}
 
@@ -120,25 +124,28 @@ def tile_picked_spconv_none_e_kernel(tc, xT, w1_words, w1_scales, w2_words, w2_s
                 windows[d][b][:].indirect(to_sb[d][:, v0 // 16 : (v0 + n) // 16]), results[i, b][:]
             )
 
+        def as_words(woven):
+            return woven[:].rearrange("p v j -> p (v j)").bitcast(U32)
+
         woven0 = keep.tile([P, 128, PACK], BF16, name="woven0", align_bytes=64)
         woven1 = keep.tile([P, 256, PACK], BF16, name="woven1", align_bytes=64)
-        weave(woven0, 0, picked[:, 0:2, 256:384])
-        weave(woven1, 0, picked[:, 0:2, 0:256])
-        gather(picked[:, 3, 256:384], 3, 256, 128)
-        gather(picked[:, 3, 0:256], 3, 0, 256)
-        weave(woven0, 2, picked[:, 2:4, 256:384])
-        weave(woven1, 2, picked[:, 2:4, 0:256])
+        gather(3, 128, 128, 1)
+        gather(3, 256, 256, 2)
+        weave(as_words(woven0).rearrange("p (v u) -> p v u", u=2), chunks[:, 2:4, :].rearrange("p u v -> p v u"))
+        weave(
+            as_words(woven1).rearrange("p (q v u) -> p q v u", q=2, u=2),
+            chunks[:, 4:8, :].rearrange("p (q u) v -> p q v u", u=2),
+        )
         quantize(0, woven0)
-        gather(picked[:, 2, 256:384], 2, 384, 128)
-        gather(picked[:, 3, 256:384], 3, 384, 128)
+        gather(2, 0, 128, 1)
+        gather(3, 0, 128, 1)
         quantize(1, woven1)
         accs0 = product(0)
         accs1 = product(1)
         drain(0, 0, accs0, "y0_0")
         drain(0, 1, accs0, "y0_1")
         woven2 = keep.tile([P, 128, PACK], BF16, name="woven2", tag="scales0", align_bytes=64)
-        weave(woven2, 0, picked[:, 0:2, 384:512])
-        weave(woven2, 2, picked[:, 2:4, 256:384])
+        weave(as_words(woven2).rearrange("p (v u) -> p v u", u=2), chunks[:, 0:4:3, :].rearrange("p u v -> p v u"))
         scatter(0, 0)
         scatter(0, 1)
         quantize(2, woven2)
@@ -163,9 +170,9 @@ def tile_picked_spconv_none_e_kernel(tc, xT, w1_words, w1_scales, w2_words, w2_s
             )
 
         for c in range(4):
-            turn(c, 0, True)
+            turn(c, 1, True)
         for c in range(4):
-            turn(c, 1, False)
+            turn(c, 0, False)
         summed = []
         for c in range(4):
             summed.append(keep.tile([P, P], F32, name="summed%d" % c))

@@ -14,6 +14,7 @@ U16 = mybir.dt.uint16
 U8 = mybir.dt.uint8
 FP8X4 = mybir.dt.float8_e4m3fn_x4
 ADD = mybir.AluOpType.add
+COPY = mybir.ActivationFunctionType.Copy
 
 P = 128
 PACK = 4
@@ -77,8 +78,11 @@ def tile_picked_spconv_none_e_kernel(tc, xT, w1_words, w1_scales, w2_words, w2_s
                 planes[j][:].indirect(offs_sb[:, e0 // 16 : (e0 + n) // 16]),
             )
 
-        gather(0, 0, 512, 0)
-        gather(1, 0, 512, 0)
+        for j in range(2):
+            gather(j, 128, 384, 1)
+            rounded = keep.tile([P, T], BF16, name="rounded%d" % j)
+            nc.scalar.activation(rounded[:], planes[j][:], COPY)
+            nc.scalar.activation(pairs[:, 0, 0, :, j], rounded[:].indirect(offs_sb[:, 0:8]), COPY)
         gather(2, 128, 384, 1)
 
         def weave(woven, words):

@@ -20,7 +20,6 @@ P = 128
 PACK = 4
 TAPS = 2
 BLOCKS = N // P
-PIECES = ((0, 128, 128), (1, 0, 256), (0, 0, 128))
 
 
 def tile_picked_spconv_none_e_kernel(tc, xT, w1_words, w1_scales, w2_words, w2_scales, offs, to1, to2, out):
@@ -45,11 +44,7 @@ def tile_picked_spconv_none_e_kernel(tc, xT, w1_words, w1_scales, w2_words, w2_s
                 )
 
         def load_words(d, words):
-            for b in range(BLOCKS):
-                m = slice(b * P, (b + 1) * P)
-                nc.sync.dma_start(
-                    out=w_words[d][:, m].bitcast(I32), in_=words[0, :, m, :].rearrange("p n t -> p (n t)").bitcast(I32)
-                )
+            nc.sync.dma_start(out=w_words[d][:].bitcast(I32), in_=words[0].rearrange("p n t -> p (n t)").bitcast(I32))
 
         nc.sync.dma_start(out=planes[0][:], in_=x_rows[0])
         nc.sync.dma_start(offs_sb[:], offs)
@@ -59,8 +54,8 @@ def tile_picked_spconv_none_e_kernel(tc, xT, w1_words, w1_scales, w2_words, w2_s
         load_scales(0, w1_scales)
         nc.sync.dma_start(to_sb[0][:], to1)
         load_words(1, w2_words)
-        nc.sync.dma_start(to_sb[1][:], to2)
         load_scales(1, w2_scales)
+        nc.sync.dma_start(to_sb[1][:], to2)
 
         windows = [[keep.tile([P, U], F32, name="window%d_%d" % (d, b)) for b in range(BLOCKS)] for d in range(TAPS)]
         for d in range(TAPS):
@@ -88,80 +83,88 @@ def tile_picked_spconv_none_e_kernel(tc, xT, w1_words, w1_scales, w2_words, w2_s
         def weave(woven, words):
             nc.scalar.copy(out=woven, in_=words)
 
-        codes, scales, results = {}, {}, {}
-
-        def quantize(i, woven):
-            n = PIECES[i][2]
-            codes[i] = keep.tile([P, n], U32, name="codes%d" % i, tag="codes%d" % i, align_bytes=64)
-            scales[i] = keep.tile([P, n], U8, name="scales%d" % i, tag="scales%d" % min(i, 1), align_bytes=64)
+        def quantize(codes, scales, woven, v0, n):
             nc.vector.quantize_mx(
-                out=codes[i][:].bitcast(FP8X4), scales=scales[i][:], in_=woven[:].rearrange("p v j -> p (v j)")
+                out=codes[:, v0 : v0 + n].bitcast(FP8X4),
+                scales=scales[:, v0 : v0 + n],
+                in_=woven[:, v0 : v0 + n, :].rearrange("p v j -> p (v j)"),
             )
 
-        def product(i):
-            d, v0, n = PIECES[i]
-            accs = []
-            for b in range(BLOCKS):
-                acc = psum.tile([P, 512], F32, name="acc%d_%d" % (i, b), tag="acc%d_%d" % (i, b))
-                m = slice(b * P, (b + 1) * P)
-                nc.tensor.matmul_mx(
-                    out=acc[:, 0:n],
-                    lhsT=w_words[d][:, m].bitcast(FP8X4),
-                    lhsT_scale=w_scales[d][:, m],
-                    rhs=codes[i][:].bitcast(FP8X4),
-                    rhs_scale=scales[i][:],
-                    start=True,
-                    stop=True,
-                )
-                accs.append(acc)
-            return accs
-
-        def drain(i, b, accs, tag):
-            n = PIECES[i][2]
-            y = keep.tile([P, n], F32, name="y%d_%d" % (i, b), tag=tag, align_bytes=64)
-            nc.scalar.copy(out=y[:], in_=accs[b][:, 0:n])
-            results[i, b] = y
-
-        def scatter(i, b):
-            d, v0, n = PIECES[i]
-            nc.vector.tensor_copy(
-                windows[d][b][:].indirect(to_sb[d][:, v0 // 16 : (v0 + n) // 16]), results[i, b][:]
+        def product(acc, d, b, codes, scales):
+            m = slice(b * P, (b + 1) * P)
+            nc.tensor.matmul_mx(
+                out=acc,
+                lhsT=w_words[d][:, m].bitcast(FP8X4),
+                lhsT_scale=w_scales[d][:, m],
+                rhs=codes.bitcast(FP8X4),
+                rhs_scale=scales,
+                start=True,
+                stop=True,
             )
+
+        def drain(name, acc, n, tag):
+            y = keep.tile([P, n], F32, name=name, tag=tag, align_bytes=64)
+            nc.scalar.copy(out=y[:], in_=acc[:, 0:n])
+            return y
+
+        def scatter(d, b, v0, n, y):
+            nc.vector.tensor_copy(windows[d][b][:].indirect(to_sb[d][:, v0 // 16 : (v0 + n) // 16]), y[:])
 
         def as_words(woven):
-            return woven[:].rearrange("p v j -> p (v j)").bitcast(U32)
+            return woven[:].rearrange("p v j -> p (v j)").bitcast(U32).rearrange("p (v u) -> p v u", u=2)
+
+        def bank(name):
+            return psum.tile([P, 512], F32, name=name, tag=name)
+
+        def mx_tiles(i, n):
+            return (
+                keep.tile([P, n], U32, name="codes%d" % i, tag="codes%d" % i, align_bytes=64),
+                keep.tile([P, n], U8, name="scales%d" % i, tag="scales%d" % min(i, 1), align_bytes=64),
+            )
 
         woven0 = keep.tile([P, 128, PACK], BF16, name="woven0", align_bytes=64)
         woven1 = keep.tile([P, 256, PACK], BF16, name="woven1", align_bytes=64)
         gather(3, 128, 128, 1)
-        gather(3, 256, 256, 2)
-        weave(as_words(woven0).rearrange("p (v u) -> p v u", u=2), chunks[:, 2:4, :].rearrange("p u v -> p v u"))
-        weave(
-            as_words(woven1).rearrange("p (q v u) -> p q v u", q=2, u=2),
-            chunks[:, 4:8, :].rearrange("p (q u) v -> p q v u", u=2),
-        )
-        quantize(0, woven0)
+        gather(3, 256, 128, 2)
+        gather(3, 384, 128, 3)
+        for v0 in (64, 0):
+            weave(as_words(woven0)[:, v0 : v0 + 64, :], chunks[:, 2:4, v0 : v0 + 64].rearrange("p u v -> p v u"))
+        for h in range(2):
+            weave(
+                as_words(woven1)[:, 128 * h : 128 * h + 128, :],
+                chunks[:, 4 + 2 * h : 6 + 2 * h, :].rearrange("p u v -> p v u"),
+            )
+        codes0, scales0 = mx_tiles(0, 128)
+        quantize(codes0, scales0, woven0, 64, 64)
+        quantize(codes0, scales0, woven0, 0, 64)
         gather(2, 0, 128, 1)
         gather(3, 0, 128, 1)
-        quantize(1, woven1)
-        accs0 = product(0)
-        accs1 = product(1)
-        drain(0, 0, accs0, "y0_0")
-        drain(0, 1, accs0, "y0_1")
+        codes1, scales1 = mx_tiles(1, 256)
+        quantize(codes1, scales1, woven1, 0, 256)
+        acc00, acc01, acc10, acc11, acc20, acc21 = [bank("acc%d_%d" % (i, b)) for i in range(3) for b in range(2)]
+        product(acc00[:, 0:64], 0, 0, codes0[:, 64:128], scales0[:, 64:128])
+        product(acc01[:, 0:128], 0, 1, codes0[:], scales0[:])
+        product(acc20[:, 128:192], 0, 0, codes0[:, 0:64], scales0[:, 0:64])
+        product(acc10[:, 0:256], 1, 0, codes1[:], scales1[:])
+        product(acc11[:, 0:256], 1, 1, codes1[:], scales1[:])
+        y00 = drain("y00", acc00, 64, "y00")
+        y01 = drain("y01", acc01, 128, "y01")
         woven2 = keep.tile([P, 128, PACK], BF16, name="woven2", tag="scales0", align_bytes=64)
-        weave(as_words(woven2).rearrange("p (v u) -> p v u", u=2), chunks[:, 0:4:3, :].rearrange("p u v -> p v u"))
-        scatter(0, 0)
-        scatter(0, 1)
-        quantize(2, woven2)
-        drain(1, 0, accs1, "y1_0")
-        accs2 = product(2)
-        scatter(1, 0)
-        drain(2, 0, accs2, "y2_0")
-        drain(2, 1, accs2, "y2_1")
-        drain(1, 1, accs1, "codes2")
-        scatter(2, 0)
-        scatter(2, 1)
-        scatter(1, 1)
+        weave(as_words(woven2), chunks[:, 0:4:3, :].rearrange("p u v -> p v u"))
+        scatter(0, 0, 192, 64, y00)
+        scatter(0, 1, 128, 128, y01)
+        codes2, scales2 = mx_tiles(2, 128)
+        quantize(codes2, scales2, woven2, 0, 128)
+        y10 = drain("y10", acc10, 256, "y10")
+        product(acc20[:, 0:128], 0, 0, codes2[:], scales2[:])
+        product(acc21[:, 0:128], 0, 1, codes2[:], scales2[:])
+        scatter(1, 0, 0, 256, y10)
+        y20 = drain("y20", acc20, 192, "y20")
+        y21 = drain("y21", acc21, 128, "y21")
+        y11 = drain("y11", acc11, 256, "codes2")
+        scatter(0, 0, 0, 192, y20)
+        scatter(0, 1, 0, 128, y21)
+        scatter(1, 1, 0, 256, y11)
 
         turned = []
         for c, tag in enumerate(("turn0", "turn1", "acc2_0", "acc1_0")):

@@ -43,17 +43,19 @@ def tile_picked_spconv_none_e_kernel(tc, xT, w1_words, w1_scales, w2_words, w2_s
                     in_=rows.unsqueeze(0).broadcast_to([8, 4, N // 4]),
                 )
 
-        def load_words(d, words):
-            nc.sync.dma_start(out=w_words[d][:].bitcast(I32), in_=words[0].rearrange("p n t -> p (n t)").bitcast(I32))
+        def load_words(d, words, m):
+            nc.sync.dma_start(
+                out=w_words[d][:, m].bitcast(I32), in_=words[0, :, m, :].rearrange("p n t -> p (n t)").bitcast(I32)
+            )
 
         nc.sync.dma_start(out=planes[0][:], in_=x_rows[0])
         nc.sync.dma_start(offs_sb[:], offs)
         for j in range(1, PACK):
             nc.sync.dma_start(out=planes[j][:], in_=x_rows[j])
-        load_words(0, w1_words)
+        load_words(0, w1_words, slice(0, N))
         load_scales(0, w1_scales)
         nc.sync.dma_start(to_sb[0][:], to1)
-        load_words(1, w2_words)
+        load_words(1, w2_words, slice(0, N))
         load_scales(1, w2_scales)
         nc.sync.dma_start(to_sb[1][:], to2)
 
@@ -190,9 +192,11 @@ def tile_picked_spconv_none_e_kernel(tc, xT, w1_words, w1_scales, w2_words, w2_s
                 nc.tensor.transpose(back[:, c * P : (c + 1) * P], summed[2 * h + c][:], ident[:])
             first = keep.tile([P, U // 2], F32, name="first%d" % h)
             nc.scalar.copy(out=first[:], in_=back[:, 0 : U // 2])
-            nc.scalar.dma_start(out=out[0:P, h * (U // 2) : (h + 1) * (U // 2)], in_=first[:])
-        for h in range(2):
-            cols = slice(h * (U // 2), (h + 1) * (U // 2))
-            half = keep.tile([P, U // 2], F32, name="half%d" % h)
+            for c in range(2):
+                u0 = (2 * h + c) * P
+                nc.scalar.dma_start(out=out[0:P, u0 : u0 + P], in_=first[:, c * P : (c + 1) * P])
+        for h, (u0, n) in enumerate(((0, 192), (192, 192), (384, 128))):
+            cols = slice(u0, u0 + n)
+            half = keep.tile([P, n], F32, name="half%d" % h)
             nc.vector.tensor_tensor(half[:], windows[0][1][:, cols], windows[1][1][:, cols], ADD)
             nc.sync.dma_start(out=out[P : 2 * P, cols], in_=half[:])

@@ -20,6 +20,14 @@ P = 128
 PACK = 4
 TAPS = 2
 BLOCKS = N // P
+COLUMN = 16
+BANK = 512
+G = 128
+HALF = G // 2
+
+REAR, LEAD, MIDDLE, GROUPS = 2, 3, 4, 6
+
+LAST_PARTS = ((0, 192), (192, 192), (384, 128))
 
 
 def tile_picked_spconv_none_e_kernel(tc, xT, w1_words, w1_scales, w2_words, w2_scales, offs, to1, to2, out):
@@ -28,8 +36,8 @@ def tile_picked_spconv_none_e_kernel(tc, xT, w1_words, w1_scales, w2_words, w2_s
         keep = ctx.enter_context(tc.tile_pool(name="keep", bufs=1))
         psum = ctx.enter_context(tc.psum_pool(name="psum", bufs=1))
 
-        offs_sb = keep.tile([P, TAPS * V // 16], U16, name="offs_sb")
-        to_sb = [keep.tile([P, V // 16], U16, name="to%d" % d) for d in range(TAPS)]
+        offs_sb = keep.tile([P, TAPS * V // COLUMN], U16, name="offs_sb")
+        to_sb = [keep.tile([P, V // COLUMN], U16, name="to%d" % d) for d in range(TAPS)]
         planes = [keep.tile([P, T], F32, name="plane%d" % j) for j in range(PACK)]
         w_words = [keep.tile([P, N], U32, name="w_words%d" % d, align_bytes=64) for d in range(TAPS)]
         w_scales = [keep.tile([P, N], U8, name="w_scales%d" % d, align_bytes=64) for d in range(TAPS)]
@@ -43,19 +51,17 @@ def tile_picked_spconv_none_e_kernel(tc, xT, w1_words, w1_scales, w2_words, w2_s
                     in_=rows.unsqueeze(0).broadcast_to([8, 4, N // 4]),
                 )
 
-        def load_words(d, words, m):
-            nc.sync.dma_start(
-                out=w_words[d][:, m].bitcast(I32), in_=words[0, :, m, :].rearrange("p n t -> p (n t)").bitcast(I32)
-            )
+        def load_words(d, words):
+            nc.sync.dma_start(out=w_words[d][:].bitcast(I32), in_=words[0].rearrange("p n t -> p (n t)").bitcast(I32))
 
         nc.sync.dma_start(out=planes[0][:], in_=x_rows[0])
         nc.sync.dma_start(offs_sb[:], offs)
-        for j in range(1, PACK):
+        for j in (2, 1, 3):
             nc.sync.dma_start(out=planes[j][:], in_=x_rows[j])
-        load_words(0, w1_words, slice(0, N))
         load_scales(0, w1_scales)
+        load_words(0, w1_words)
         nc.sync.dma_start(to_sb[0][:], to1)
-        load_words(1, w2_words, slice(0, N))
+        load_words(1, w2_words)
         load_scales(1, w2_scales)
         nc.sync.dma_start(to_sb[1][:], to2)
 
@@ -66,24 +72,36 @@ def tile_picked_spconv_none_e_kernel(tc, xT, w1_words, w1_scales, w2_words, w2_s
 
         ident = keep.tile([P, P], F32, name="ident")
         make_identity(nc, ident[:])
-        pairs = keep.tile([P, 4, 2, 128, 2], BF16, name="pairs")
-        chunks = pairs[:].rearrange("p q u v e -> p (q u v e)").bitcast(U32).rearrange("p (c v) -> p c v", v=128)
 
-        def gather(j, e0, n, q0):
+        pairs = keep.tile([P, GROUPS, 2, G, 2], BF16, name="pairs")
+        pair_values = pairs[:].rearrange("p g u v e -> p (g u v e)")
+        pair_words = pair_values.bitcast(U32).rearrange("p (c v) -> p c v", v=G)
+
+        def gather(j, first, n, g):
             nc.vector.tensor_copy(
-                pairs[:, q0 : q0 + n // 128, j // 2, :, j % 2],
-                planes[j][:].indirect(offs_sb[:, e0 // 16 : (e0 + n) // 16]),
+                pairs[:, g : g + n // G, j // 2, :, j % 2],
+                planes[j][:].indirect(offs_sb[:, first // COLUMN : (first + n) // COLUMN]),
             )
 
         for j in range(2):
-            gather(j, 128, 384, 1)
+            gather(j, G, 3 * G, LEAD)
+            if j == 0:
+                gather(2, 0, 4 * G, REAR)
             rounded = keep.tile([P, T], BF16, name="rounded%d" % j)
             nc.scalar.activation(rounded[:], planes[j][:], COPY)
-            nc.scalar.activation(pairs[:, 0, 0, :, j], rounded[:].indirect(offs_sb[:, 0:8]), COPY)
-        gather(2, 128, 384, 1)
+            nc.scalar.activation(pairs[:, j, 0, :, j], rounded[:].indirect(offs_sb[:, 0 : G // COLUMN]), COPY)
 
-        def weave(woven, words):
-            nc.scalar.copy(out=woven, in_=words)
+        def weave_words(woven, v0, n, g, g_v0):
+            target = woven[:].rearrange("p v j -> p (v j)").bitcast(U32).rearrange("p (v u) -> p v u", u=2)
+            nc.scalar.copy(
+                out=target[:, v0 : v0 + n, :],
+                in_=pair_words[:, 2 * g : 2 * g + 2, g_v0 : g_v0 + n].rearrange("p u v -> p v u"),
+            )
+
+        def mx_tiles(piece, n, scales_tag):
+            codes = keep.tile([P, n], U32, name="codes_" + piece, tag="codes_" + piece, align_bytes=64)
+            scales = keep.tile([P, n], U8, name="scales_" + piece, tag=scales_tag, align_bytes=64)
+            return codes, scales
 
         def quantize(codes, scales, woven, v0, n):
             nc.vector.quantize_mx(
@@ -104,99 +122,90 @@ def tile_picked_spconv_none_e_kernel(tc, xT, w1_words, w1_scales, w2_words, w2_s
                 stop=True,
             )
 
-        def drain(name, acc, n, tag):
+        def drain(acc, n, name, tag):
             y = keep.tile([P, n], F32, name=name, tag=tag, align_bytes=64)
             nc.scalar.copy(out=y[:], in_=acc[:, 0:n])
             return y
 
         def scatter(d, b, v0, n, y):
-            nc.vector.tensor_copy(windows[d][b][:].indirect(to_sb[d][:, v0 // 16 : (v0 + n) // 16]), y[:])
+            nc.vector.tensor_copy(windows[d][b][:].indirect(to_sb[d][:, v0 // COLUMN : (v0 + n) // COLUMN]), y[:])
 
-        def as_words(woven):
-            return woven[:].rearrange("p v j -> p (v j)").bitcast(U32).rearrange("p (v u) -> p v u", u=2)
-
-        def bank(name):
-            return psum.tile([P, 512], F32, name=name, tag=name)
-
-        def mx_tiles(i, n):
-            return (
-                keep.tile([P, n], U32, name="codes%d" % i, tag="codes%d" % i, align_bytes=64),
-                keep.tile([P, n], U8, name="scales%d" % i, tag="scales%d" % min(i, 1), align_bytes=64),
-            )
-
-        woven0 = keep.tile([P, 128, PACK], BF16, name="woven0", align_bytes=64)
-        woven1 = keep.tile([P, 256, PACK], BF16, name="woven1", align_bytes=64)
-        gather(3, 128, 128, 1)
-        gather(3, 256, 128, 2)
-        gather(3, 384, 128, 3)
-        for v0 in (64, 0):
-            weave(as_words(woven0)[:, v0 : v0 + 64, :], chunks[:, 2:4, v0 : v0 + 64].rearrange("p u v -> p v u"))
+        woven_lead = keep.tile([P, G, PACK], BF16, name="woven_lead", align_bytes=64)
+        woven_middle = keep.tile([P, V, PACK], BF16, name="woven_middle", align_bytes=64)
+        gather(3, G, G, LEAD)
         for h in range(2):
-            weave(
-                as_words(woven1)[:, 128 * h : 128 * h + 128, :],
-                chunks[:, 4 + 2 * h : 6 + 2 * h, :].rearrange("p u v -> p v u"),
-            )
-        codes0, scales0 = mx_tiles(0, 128)
-        quantize(codes0, scales0, woven0, 64, 64)
-        quantize(codes0, scales0, woven0, 0, 64)
-        gather(2, 0, 128, 1)
-        gather(3, 0, 128, 1)
-        codes1, scales1 = mx_tiles(1, 256)
-        quantize(codes1, scales1, woven1, 0, 256)
-        acc00, acc01, acc10, acc11, acc20, acc21 = [bank("acc%d_%d" % (i, b)) for i in range(3) for b in range(2)]
-        product(acc00[:, 0:64], 0, 0, codes0[:, 64:128], scales0[:, 64:128])
-        product(acc01[:, 0:128], 0, 1, codes0[:], scales0[:])
-        product(acc20[:, 128:192], 0, 0, codes0[:, 0:64], scales0[:, 0:64])
-        product(acc10[:, 0:256], 1, 0, codes1[:], scales1[:])
-        product(acc11[:, 0:256], 1, 1, codes1[:], scales1[:])
-        y00 = drain("y00", acc00, 64, "y00")
-        y01 = drain("y01", acc01, 128, "y01")
-        woven2 = keep.tile([P, 128, PACK], BF16, name="woven2", tag="scales0", align_bytes=64)
-        weave(as_words(woven2), chunks[:, 0:4:3, :].rearrange("p u v -> p v u"))
-        scatter(0, 0, 192, 64, y00)
-        scatter(0, 1, 128, 128, y01)
-        codes2, scales2 = mx_tiles(2, 128)
-        quantize(codes2, scales2, woven2, 0, 128)
-        y10 = drain("y10", acc10, 256, "y10")
-        product(acc20[:, 0:128], 0, 0, codes2[:], scales2[:])
-        product(acc21[:, 0:128], 0, 1, codes2[:], scales2[:])
-        scatter(1, 0, 0, 256, y10)
-        y20 = drain("y20", acc20, 192, "y20")
-        y21 = drain("y21", acc21, 128, "y21")
-        y11 = drain("y11", acc11, 256, "codes2")
-        scatter(0, 0, 0, 192, y20)
-        scatter(0, 1, 0, 128, y21)
-        scatter(1, 1, 0, 256, y11)
+            gather(3, V + h * G, G, MIDDLE + h)
+        for v0 in (HALF, 0):
+            weave_words(woven_lead, v0, HALF, LEAD, v0)
+        for h in range(2):
+            weave_words(woven_middle, h * G, G, MIDDLE + h, 0)
+        codes_lead, scales_lead = mx_tiles("lead", G, "scales_lead")
+        for v0 in (HALF, 0):
+            quantize(codes_lead, scales_lead, woven_lead, v0, HALF)
+        gather(3, 0, G, LEAD)
+        codes_middle, scales_middle = mx_tiles("middle", V, "scales_middle")
+        quantize(codes_middle, scales_middle, woven_middle, 0, V)
+
+        acc = {}
+        for piece in ("lead", "middle", "rear"):
+            for b in range(BLOCKS):
+                name = "acc_%s%d" % (piece, b)
+                acc[piece, b] = psum.tile([P, BANK], F32, name=name, tag=name)
+        product(acc["lead", 0][:, 0:HALF], 0, 0, codes_lead[:, HALF:G], scales_lead[:, HALF:G])
+        product(acc["lead", 1][:, 0:G], 0, 1, codes_lead[:], scales_lead[:])
+        product(acc["rear", 0][:, G : G + HALF], 0, 0, codes_lead[:, 0:HALF], scales_lead[:, 0:HALF])
+        for b in range(BLOCKS):
+            product(acc["middle", b][:, 0:V], 1, b, codes_middle[:], scales_middle[:])
+        y_lead0 = drain(acc["lead", 0], HALF, "y_lead0", "y_lead0")
+        y_lead1 = drain(acc["lead", 1], G, "y_lead1", "y_lead1")
+
+        row = 2 * G
+        step_a, step_b = (2 * REAR + 1) * row, 2 * row + 1
+        woven_rear = keep.tile([P, G, PACK], BF16, name="woven_rear", tag="scales_lead", align_bytes=64)
+        rear = pair_values[:, 0 : 2 * step_a].rearrange("p (a r) -> p a r", a=2)
+        rear = rear[:, :, 0 : 2 * step_b].rearrange("p a (b r) -> p a b r", b=2)[:, :, :, 0:row:2]
+        nc.scalar.copy(out=woven_rear[:].rearrange("p v (a b) -> p v a b", a=2), in_=rear.rearrange("p a b v -> p v a b"))
+
+        scatter(0, 0, G + HALF, HALF, y_lead0)
+        scatter(0, 1, G, G, y_lead1)
+        codes_rear, scales_rear = mx_tiles("rear", G, "scales_middle")
+        quantize(codes_rear, scales_rear, woven_rear, 0, G)
+        y_middle0 = drain(acc["middle", 0], V, "y_middle0", "y_middle0")
+        for b in range(BLOCKS):
+            product(acc["rear", b][:, 0:G], 0, b, codes_rear[:], scales_rear[:])
+        scatter(1, 0, 0, V, y_middle0)
+        y_rear0 = drain(acc["rear", 0], G + HALF, "y_rear0", "y_rear0")
+        y_rear1 = drain(acc["rear", 1], G, "y_rear1", "y_rear1")
+        y_middle1 = drain(acc["middle", 1], V, "y_middle1", "codes_rear")
+        scatter(0, 0, 0, G + HALF, y_rear0)
+        scatter(0, 1, 0, G, y_rear1)
+        scatter(1, 1, 0, V, y_middle1)
 
         turned = []
-        for c, tag in enumerate(("turn0", "turn1", "acc2_0", "acc1_0")):
-            turned.append(psum.tile([P, 512], F32, name="turn%d" % c, tag=tag))
-
-        def turn(c, d, start):
-            nc.tensor.matmul(
-                turned[c][:, 0:P], windows[d][0][:, c * P : (c + 1) * P], ident[:],
-                start=start, stop=not start, is_transpose=True,
-            )
-
-        for c in range(4):
-            turn(c, 1, True)
-        for c in range(4):
-            turn(c, 0, False)
+        for c, tag in enumerate(("turn0", "turn1", "acc_rear0", "acc_middle0")):
+            turned.append(psum.tile([P, BANK], F32, name="turn%d" % c, tag=tag))
+        for d, start in ((1, True), (0, False)):
+            for c in range(U // P):
+                nc.tensor.matmul(
+                    turned[c][:, 0:P], windows[d][0][:, c * P : (c + 1) * P], ident[:],
+                    start=start, stop=not start, is_transpose=True,
+                )
         summed = []
-        for c in range(4):
+        for c in range(U // P):
             summed.append(keep.tile([P, P], F32, name="summed%d" % c))
             nc.scalar.copy(out=summed[c][:], in_=turned[c][:, 0:P])
-        for h, tag in enumerate(("acc0_0", "acc0_1")):
-            back = psum.tile([P, 512], F32, name="back%d" % h, tag=tag)
+        for h, tag in enumerate(("acc_lead0", "acc_lead1")):
+            back = psum.tile([P, BANK], F32, name="back%d" % h, tag=tag)
             for c in range(2):
                 nc.tensor.transpose(back[:, c * P : (c + 1) * P], summed[2 * h + c][:], ident[:])
-            first = keep.tile([P, U // 2], F32, name="first%d" % h)
-            nc.scalar.copy(out=first[:], in_=back[:, 0 : U // 2])
+            upper = keep.tile([P, U // 2], F32, name="upper%d" % h)
+            nc.scalar.copy(out=upper[:], in_=back[:, 0 : U // 2])
             for c in range(2):
                 u0 = (2 * h + c) * P
-                nc.scalar.dma_start(out=out[0:P, u0 : u0 + P], in_=first[:, c * P : (c + 1) * P])
-        for h, (u0, n) in enumerate(((0, 192), (192, 192), (384, 128))):
+                nc.scalar.dma_start(out=out[0:P, u0 : u0 + P], in_=upper[:, c * P : (c + 1) * P])
+
+        for h, (u0, n) in enumerate(LAST_PARTS):
             cols = slice(u0, u0 + n)
-            half = keep.tile([P, n], F32, name="half%d" % h)
-            nc.vector.tensor_tensor(half[:], windows[0][1][:, cols], windows[1][1][:, cols], ADD)
-            nc.sync.dma_start(out=out[P : 2 * P, cols], in_=half[:])
+            lower = keep.tile([P, n], F32, name="lower%d" % h)
+            nc.vector.tensor_tensor(lower[:], windows[0][1][:, cols], windows[1][1][:, cols], ADD)
+            nc.sync.dma_start(out=out[P : 2 * P, cols], in_=lower[:])

@@ -192,7 +192,7 @@ def tile_picked_spconv_none_e_kernel(tc, xT, w1_words, w1_scales, w2_words, w2_s
                 )
         summed = []
         for c in range(U // P):
-            summed.append(keep.tile([P, P], F32, name="summed%d" % c))
+            summed.append(keep.tile([P, P], F32, name="summed%d" % c, tag="summed%d" % c))
             nc.scalar.copy(out=summed[c][:], in_=turned[c][:, 0:P])
         for h, tag in enumerate(("acc_lead0", "acc_lead1")):
             back = psum.tile([P, BANK], F32, name="back%d" % h, tag=tag)
@@ -202,10 +202,10 @@ def tile_picked_spconv_none_e_kernel(tc, xT, w1_words, w1_scales, w2_words, w2_s
             nc.scalar.copy(out=upper[:], in_=back[:, 0 : U // 2])
             for c in range(2):
                 u0 = (2 * h + c) * P
-                nc.scalar.dma_start(out=out[0:P, u0 : u0 + P], in_=upper[:, c * P : (c + 1) * P])
+                nc.sync.dma_start(out=out[0:P, u0 : u0 + P], in_=upper[:, c * P : (c + 1) * P])
 
-        for h, (u0, n) in enumerate(LAST_PARTS):
+        lower = keep.tile([P, U], F32, name="lower", tag="summed3")
+        for u0, n in LAST_PARTS:
             cols = slice(u0, u0 + n)
-            lower = keep.tile([P, n], F32, name="lower%d" % h)
-            nc.vector.tensor_tensor(lower[:], windows[0][1][:, cols], windows[1][1][:, cols], ADD)
-            nc.sync.dma_start(out=out[P : 2 * P, cols], in_=lower[:])
+            nc.vector.tensor_tensor(lower[:, cols], windows[0][1][:, cols], windows[1][1][:, cols], ADD)
+            nc.sync.dma_start(out=out[P : 2 * P, cols], in_=lower[:, cols])

@@ -27,7 +27,7 @@ HALF = G // 2
 
 REAR, LEAD, MIDDLE, GROUPS = 2, 3, 4, 6
 
-LAST_PARTS = ((0, 192), (192, 192), (384, 128))
+LAST_PARTS = ((0, 128), (128, 192), (320, 192))
 
 
 def tile_picked_spconv_none_e_kernel(tc, xT, w1_words, w1_scales, w2_words, w2_scales, offs, to1, to2, out):
@@ -194,15 +194,12 @@ def tile_picked_spconv_none_e_kernel(tc, xT, w1_words, w1_scales, w2_words, w2_s
         for c in range(U // P):
             summed.append(keep.tile([P, P], F32, name="summed%d" % c, tag="summed%d" % c))
             nc.scalar.copy(out=summed[c][:], in_=turned[c][:, 0:P])
-        for h, tag in enumerate(("acc_lead0", "acc_lead1")):
-            back = psum.tile([P, BANK], F32, name="back%d" % h, tag=tag)
-            for c in range(2):
-                nc.tensor.transpose(back[:, c * P : (c + 1) * P], summed[2 * h + c][:], ident[:])
-            upper = keep.tile([P, U // 2], F32, name="upper%d" % h)
-            nc.scalar.copy(out=upper[:], in_=back[:, 0 : U // 2])
-            for c in range(2):
-                u0 = (2 * h + c) * P
-                nc.sync.dma_start(out=out[0:P, u0 : u0 + P], in_=upper[:, c * P : (c + 1) * P])
+        for c, tag in enumerate(("acc_lead0", "acc_lead1", "turn0", "turn1")):
+            back = psum.tile([P, BANK], F32, name="back%d" % c, tag=tag)
+            nc.tensor.transpose(back[:, 0:P], summed[c][:], ident[:])
+            upper = keep.tile([P, P], F32, name="upper%d" % c)
+            nc.scalar.copy(out=upper[:], in_=back[:, 0:P])
+            nc.sync.dma_start(out=out[0:P, c * P : (c + 1) * P], in_=upper[:])
 
         lower = keep.tile([P, U], F32, name="lower", tag="summed3")
         for u0, n in LAST_PARTS:

@@ -198,7 +198,10 @@ def tile_picked_spconv_none_e_kernel(tc, xT, w1_words, w1_scales, w2_words, w2_s
             back = psum.tile([P, BANK], F32, name="back%d" % c, tag=tag)
             nc.tensor.transpose(back[:, 0:P], summed[c][:], ident[:])
             upper = keep.tile([P, P], F32, name="upper%d" % c)
-            nc.scalar.copy(out=upper[:], in_=back[:, 0:P])
+            if c < U // P - 1:
+                nc.scalar.copy(out=upper[:], in_=back[:, 0:P])
+            else:
+                nc.vector.tensor_copy(upper[:], back[:, 0:P])
             nc.sync.dma_start(out=out[0:P, c * P : (c + 1) * P], in_=upper[:])
 
         lower = keep.tile([P, U], F32, name="lower", tag="summed3")

@@ -1,7 +1,6 @@
 from contextlib import ExitStack
 
 import concourse.mybir as mybir
-from concourse.masks import make_identity
 
 K, T, V, N, U = 512, 1024, 256, 256, 512
 FLOPS = 2 * 2 * K * V * N
@@ -23,9 +22,6 @@ BLOCKS = N // P
 COLUMN = 16
 BANK = 512
 G = 128
-HALF = G // 2
-
-REAR, LEAD, MIDDLE, GROUPS = 2, 3, 4, 6
 
 LAST_PARTS = ((0, 128), (128, 192), (320, 192))
 
@@ -43,10 +39,10 @@ def tile_picked_spconv_none_e_kernel(tc, xT, w1_words, w1_scales, w2_words, w2_s
         w_scales = [keep.tile([P, N], U8, name="w_scales%d" % d, align_bytes=64) for d in range(TAPS)]
         x_rows = xT.rearrange("(p j) t -> j p t", j=PACK)
 
-        def load_scales(d, scales):
+        def load_scales(d, scales, queue):
             for q in range(4):
                 rows = scales[0, 4 * q : 4 * q + 4, :].bitcast(I32)
-                nc.sync.dma_start(
+                queue.dma_start(
                     out=w_scales[d][32 * q : 32 * q + 32, :].bitcast(I32),
                     in_=rows.unsqueeze(0).broadcast_to([8, 4, N // 4]),
                 )
@@ -56,155 +52,110 @@ def tile_picked_spconv_none_e_kernel(tc, xT, w1_words, w1_scales, w2_words, w2_s
 
         nc.sync.dma_start(out=planes[0][:], in_=x_rows[0])
         nc.sync.dma_start(offs_sb[:], offs)
-        for j in (2, 1, 3):
+        load_scales(0, w1_scales, nc.sync)
+        for j in (1, 2, 3):
             nc.sync.dma_start(out=planes[j][:], in_=x_rows[j])
-        load_scales(0, w1_scales)
-        load_words(0, w1_words)
         nc.sync.dma_start(to_sb[0][:], to1)
+        load_words(0, w1_words)
         load_words(1, w2_words)
-        load_scales(1, w2_scales)
+        load_scales(1, w2_scales, nc.sync)
         nc.sync.dma_start(to_sb[1][:], to2)
 
         windows = [[keep.tile([P, U], F32, name="window%d_%d" % (d, b)) for b in range(BLOCKS)] for d in range(TAPS)]
-        for d in range(TAPS):
-            for b in range(BLOCKS):
-                nc.vector.memset(windows[d][b][:], 0.0)
+        for b in range(BLOCKS):
+            nc.vector.memset(windows[0][b][:], 0.0)
+            nc.scalar.activation(windows[1][b][:], windows[0][b][:], COPY)
 
-        ident = keep.tile([P, P], F32, name="ident")
-        make_identity(nc, ident[:])
+        def entries(first, n):
+            return offs_sb[:, first // COLUMN : (first + n) // COLUMN]
 
-        pairs = keep.tile([P, GROUPS, 2, G, 2], BF16, name="pairs")
-        pair_values = pairs[:].rearrange("p g u v e -> p (g u v e)")
-        pair_words = pair_values.bitcast(U32).rearrange("p (c v) -> p c v", v=G)
+        pairs = [keep.tile([P, 2, G, 2], BF16, name="pairs%d" % g) for g in range(2)]
+        rows = [keep.tile([P, PACK, G], BF16, name="rows%d" % g) for g in range(2)]
+        for j in range(PACK):
+            for g in range(2):
+                nc.vector.tensor_copy(pairs[g][:, j // 2, :, j % 2], planes[j][:].indirect(entries(g * G, G)))
+                nc.scalar.activation(rows[g][:, j, :], planes[j][:].indirect(entries(V + g * G, G)), COPY)
 
-        def gather(j, first, n, g):
-            nc.vector.tensor_copy(
-                pairs[:, g : g + n // G, j // 2, :, j % 2],
-                planes[j][:].indirect(offs_sb[:, first // COLUMN : (first + n) // COLUMN]),
-            )
+        woven = [keep.tile([P, G, PACK], BF16, name="woven%d" % g, align_bytes=64) for g in range(4)]
+        codes = [keep.tile([P, G], U32, name="codes%d" % g, align_bytes=64) for g in range(4)]
+        scales = [keep.tile([P, G], U8, name="scales%d" % g, align_bytes=64) for g in range(4)]
 
-        for j in range(2):
-            gather(j, G, 3 * G, LEAD)
-            if j == 0:
-                gather(2, 0, 4 * G, REAR)
-            rounded = keep.tile([P, T], BF16, name="rounded%d" % j)
-            nc.scalar.activation(rounded[:], planes[j][:], COPY)
-            nc.scalar.activation(pairs[:, j, 0, :, j], rounded[:].indirect(offs_sb[:, 0 : G // COLUMN]), COPY)
+        def word_views(g):
+            target = woven[g][:].rearrange("p v j -> p (v j)").bitcast(I32).rearrange("p (v u) -> p v u", u=2)
+            source = pairs[g][:].rearrange("p u v e -> p (u v e)").bitcast(I32).rearrange("p (u v) -> p v u", u=2)
+            return target, source
 
-        def weave_words(woven, v0, n, g, g_v0):
-            target = woven[:].rearrange("p v j -> p (v j)").bitcast(U32).rearrange("p (v u) -> p v u", u=2)
-            nc.scalar.copy(
-                out=target[:, v0 : v0 + n, :],
-                in_=pair_words[:, 2 * g : 2 * g + 2, g_v0 : g_v0 + n].rearrange("p u v -> p v u"),
-            )
+        def weave_rows(g):
+            nc.vector.tensor_copy(woven[g][:], rows[g - 2][:].rearrange("p j v -> p v j"))
 
-        def mx_tiles(piece, n, scales_tag):
-            codes = keep.tile([P, n], U32, name="codes_" + piece, tag="codes_" + piece, align_bytes=64)
-            scales = keep.tile([P, n], U8, name="scales_" + piece, tag=scales_tag, align_bytes=64)
-            return codes, scales
+        def quantize(g):
+            nc.vector.quantize_mx(out=codes[g][:].bitcast(FP8X4), scales=scales[g][:], in_=woven[g][:].rearrange("p v j -> p (v j)"))
 
-        def quantize(codes, scales, woven, v0, n):
-            nc.vector.quantize_mx(
-                out=codes[:, v0 : v0 + n].bitcast(FP8X4),
-                scales=scales[:, v0 : v0 + n],
-                in_=woven[:, v0 : v0 + n, :].rearrange("p v j -> p (v j)"),
-            )
-
-        def product(acc, d, b, codes, scales):
+        def product(g, b, acc):
+            d = g // 2
             m = slice(b * P, (b + 1) * P)
             nc.tensor.matmul_mx(
                 out=acc,
                 lhsT=w_words[d][:, m].bitcast(FP8X4),
                 lhsT_scale=w_scales[d][:, m],
-                rhs=codes.bitcast(FP8X4),
-                rhs_scale=scales,
+                rhs=codes[g][:].bitcast(FP8X4),
+                rhs_scale=scales[g][:],
                 start=True,
                 stop=True,
             )
 
-        def drain(acc, n, name, tag):
-            y = keep.tile([P, n], F32, name=name, tag=tag, align_bytes=64)
-            nc.scalar.copy(out=y[:], in_=acc[:, 0:n])
-            return y
+        target, source = word_views(0)
+        nc.vector.tensor_copy(target, source)
+        target, source = word_views(1)
+        nc.scalar.copy(out=target.bitcast(U32), in_=source.bitcast(U32))
+        weave_rows(2)
+        quantize(0)
+        weave_rows(3)
+        for g in (1, 2, 3):
+            quantize(g)
 
-        def scatter(d, b, v0, n, y):
-            nc.vector.tensor_copy(windows[d][b][:].indirect(to_sb[d][:, v0 // COLUMN : (v0 + n) // COLUMN]), y[:])
-
-        woven_lead = keep.tile([P, G, PACK], BF16, name="woven_lead", align_bytes=64)
-        woven_middle = keep.tile([P, V, PACK], BF16, name="woven_middle", align_bytes=64)
-        gather(3, G, G, LEAD)
-        for h in range(2):
-            gather(3, V + h * G, G, MIDDLE + h)
-        for v0 in (HALF, 0):
-            weave_words(woven_lead, v0, HALF, LEAD, v0)
-        for h in range(2):
-            weave_words(woven_middle, h * G, G, MIDDLE + h, 0)
-        codes_lead, scales_lead = mx_tiles("lead", G, "scales_lead")
-        for v0 in (HALF, 0):
-            quantize(codes_lead, scales_lead, woven_lead, v0, HALF)
-        gather(3, 0, G, LEAD)
-        codes_middle, scales_middle = mx_tiles("middle", V, "scales_middle")
-        quantize(codes_middle, scales_middle, woven_middle, 0, V)
-
-        acc = {}
-        for piece in ("lead", "middle", "rear"):
+        names = ("a0", "a1", "b0", "b1", "cd0", "cd1")
+        acc = {name: psum.tile([P, BANK], F32, name="acc_" + name, tag="acc_" + name) for name in names}
+        y = {name: keep.tile([P, G * (len(name) - 1)], F32, name="y_" + name) for name in names}
+        for g, name in enumerate("ab"):
             for b in range(BLOCKS):
-                name = "acc_%s%d" % (piece, b)
-                acc[piece, b] = psum.tile([P, BANK], F32, name=name, tag=name)
-        product(acc["lead", 0][:, 0:HALF], 0, 0, codes_lead[:, HALF:G], scales_lead[:, HALF:G])
-        product(acc["lead", 1][:, 0:G], 0, 1, codes_lead[:], scales_lead[:])
-        product(acc["rear", 0][:, G : G + HALF], 0, 0, codes_lead[:, 0:HALF], scales_lead[:, 0:HALF])
+                product(g, b, acc["%s%d" % (name, b)][:, 0:G])
         for b in range(BLOCKS):
-            product(acc["middle", b][:, 0:V], 1, b, codes_middle[:], scales_middle[:])
-        y_lead0 = drain(acc["lead", 0], HALF, "y_lead0", "y_lead0")
-        y_lead1 = drain(acc["lead", 1], G, "y_lead1", "y_lead1")
+            for h in range(2):
+                product(2 + h, b, acc["cd%d" % b][:, h * G : (h + 1) * G])
 
-        row = 2 * G
-        step_a, step_b = (2 * REAR + 1) * row, 2 * row + 1
-        woven_rear = keep.tile([P, G, PACK], BF16, name="woven_rear", tag="scales_lead", align_bytes=64)
-        rear = pair_values[:, 0 : 2 * step_a].rearrange("p (a r) -> p a r", a=2)
-        rear = rear[:, :, 0 : 2 * step_b].rearrange("p a (b r) -> p a b r", b=2)[:, :, :, 0:row:2]
-        nc.scalar.copy(out=woven_rear[:].rearrange("p v (a b) -> p v a b", a=2), in_=rear.rearrange("p a b v -> p v a b"))
+        def drain_s(name):
+            nc.scalar.copy(out=y[name][:], in_=acc[name][:, 0 : G * (len(name) - 1)])
 
-        scatter(0, 0, G + HALF, HALF, y_lead0)
-        scatter(0, 1, G, G, y_lead1)
-        codes_rear, scales_rear = mx_tiles("rear", G, "scales_middle")
-        quantize(codes_rear, scales_rear, woven_rear, 0, G)
-        y_middle0 = drain(acc["middle", 0], V, "y_middle0", "y_middle0")
-        for b in range(BLOCKS):
-            product(acc["rear", b][:, 0:G], 0, b, codes_rear[:], scales_rear[:])
-        scatter(1, 0, 0, V, y_middle0)
-        y_rear0 = drain(acc["rear", 0], G + HALF, "y_rear0", "y_rear0")
-        y_rear1 = drain(acc["rear", 1], G, "y_rear1", "y_rear1")
-        y_middle1 = drain(acc["middle", 1], V, "y_middle1", "codes_rear")
-        scatter(0, 0, 0, G + HALF, y_rear0)
-        scatter(0, 1, 0, G, y_rear1)
-        scatter(1, 1, 0, V, y_middle1)
+        def places(d, v0, n):
+            return to_sb[d][:, v0 // COLUMN : (v0 + n) // COLUMN]
 
-        turned = []
-        for c, tag in enumerate(("turn0", "turn1", "acc_rear0", "acc_middle0")):
-            turned.append(psum.tile([P, BANK], F32, name="turn%d" % c, tag=tag))
-        for d, start in ((1, True), (0, False)):
-            for c in range(U // P):
-                nc.tensor.matmul(
-                    turned[c][:, 0:P], windows[d][0][:, c * P : (c + 1) * P], ident[:],
-                    start=start, stop=not start, is_transpose=True,
-                )
-        summed = []
-        for c in range(U // P):
-            summed.append(keep.tile([P, P], F32, name="summed%d" % c, tag="summed%d" % c))
-            nc.scalar.copy(out=summed[c][:], in_=turned[c][:, 0:P])
-        for c, tag in enumerate(("acc_lead0", "acc_lead1", "turn0", "turn1")):
-            back = psum.tile([P, BANK], F32, name="back%d" % c, tag=tag)
-            nc.tensor.transpose(back[:, 0:P], summed[c][:], ident[:])
-            upper = keep.tile([P, P], F32, name="upper%d" % c)
-            if c < U // P - 1:
-                nc.scalar.copy(out=upper[:], in_=back[:, 0:P])
-            else:
-                nc.vector.tensor_copy(upper[:], back[:, 0:P])
-            nc.sync.dma_start(out=out[0:P, c * P : (c + 1) * P], in_=upper[:])
+        def scatter_v(d, b, v0, n, values):
+            nc.vector.tensor_copy(windows[d][b][:].indirect(places(d, v0, n)), values)
 
-        lower = keep.tile([P, U], F32, name="lower", tag="summed3")
+        def scatter_s(d, b, v0, n, values):
+            nc.scalar.activation(windows[d][b][:].indirect(places(d, v0, n)), values, COPY)
+
+        def drain_v(name):
+            nc.vector.tensor_copy(y[name][:], acc[name][:, 0 : G * (len(name) - 1)])
+
+        drain_s("a0")
+        drain_s("a1")
+        drain_v("b0")
+        scatter_s(0, 0, 0, G, y["a0"][:])
+        scatter_v(0, 1, 0, G, y["a1"][:])
+        drain_s("b1")
+        scatter_s(0, 0, G, G, y["b0"][:])
+        drain_v("cd0")
+        drain_v("cd1")
+        scatter_s(0, 1, G, G, y["b1"][:])
+        scatter_v(1, 0, 0, V, y["cd0"][:])
+        scatter_s(1, 1, 0, V, y["cd1"][:])
+
+        upper = keep.tile([P, U], F32, name="upper")
+        nc.vector.tensor_tensor(upper[:], windows[0][0][:], windows[1][0][:], ADD)
+        nc.sync.dma_start(out=out[0:P, :], in_=upper[:])
+        lower = keep.tile([P, U], F32, name="lower")
         for u0, n in LAST_PARTS:
             cols = slice(u0, u0 + n)
             nc.vector.tensor_tensor(lower[:, cols], windows[0][1][:, cols], windows[1][1][:, cols], ADD)

@@ -69,21 +69,16 @@ def tile_picked_spconv_none_e_kernel(tc, xT, w1_words, w1_scales, w2_words, w2_s
         def entries(first, n):
             return offs_sb[:, first // COLUMN : (first + n) // COLUMN]
 
-        pairs = [keep.tile([P, 2, G, 2], BF16, name="pairs%d" % g) for g in range(2)]
+        woven = [keep.tile([P, G, PACK], BF16, name="woven%d" % g, align_bytes=64) for g in range(4)]
+        codes = [keep.tile([P, G], U32, name="codes%d" % g, tag="codes%d" % g, align_bytes=64) for g in range(4)]
+        scales = [keep.tile([P, G], U8, name="scales%d" % g, align_bytes=64) for g in range(4)]
+        pairs = keep.tile([P, 2, G, 2], BF16, name="pairs")
         rows = [keep.tile([P, PACK, G], BF16, name="rows%d" % g) for g in range(2)]
         for j in range(PACK):
+            nc.vector.tensor_copy(woven[0][:, :, j], planes[j][:].indirect(entries(0, G)))
+            nc.vector.tensor_copy(pairs[:, j // 2, :, j % 2], planes[j][:].indirect(entries(G, G)))
             for g in range(2):
-                nc.vector.tensor_copy(pairs[g][:, j // 2, :, j % 2], planes[j][:].indirect(entries(g * G, G)))
                 nc.scalar.activation(rows[g][:, j, :], planes[j][:].indirect(entries(V + g * G, G)), COPY)
-
-        woven = [keep.tile([P, G, PACK], BF16, name="woven%d" % g, align_bytes=64) for g in range(4)]
-        codes = [keep.tile([P, G], U32, name="codes%d" % g, align_bytes=64) for g in range(4)]
-        scales = [keep.tile([P, G], U8, name="scales%d" % g, align_bytes=64) for g in range(4)]
-
-        def word_views(g):
-            target = woven[g][:].rearrange("p v j -> p (v j)").bitcast(I32).rearrange("p (v u) -> p v u", u=2)
-            source = pairs[g][:].rearrange("p u v e -> p (u v e)").bitcast(I32).rearrange("p (u v) -> p v u", u=2)
-            return target, source
 
         def weave_rows(g):
             nc.vector.tensor_copy(woven[g][:], rows[g - 2][:].rearrange("p j v -> p v j"))
@@ -104,28 +99,28 @@ def tile_picked_spconv_none_e_kernel(tc, xT, w1_words, w1_scales, w2_words, w2_s
                 stop=True,
             )
 
-        target, source = word_views(0)
-        nc.vector.tensor_copy(target, source)
-        target, source = word_views(1)
-        nc.scalar.copy(out=target.bitcast(U32), in_=source.bitcast(U32))
-        weave_rows(2)
         quantize(0)
+        nc.scalar.copy(
+            out=woven[1][:].rearrange("p v j -> p (v j)").bitcast(U32).rearrange("p (v u) -> p v u", u=2),
+            in_=pairs[:].rearrange("p u v e -> p (u v e)").bitcast(U32).rearrange("p (u v) -> p v u", u=2),
+        )
+        weave_rows(2)
         weave_rows(3)
         for g in (1, 2, 3):
             quantize(g)
 
-        names = ("a0", "a1", "b0", "b1", "cd0", "cd1")
-        acc = {name: psum.tile([P, BANK], F32, name="acc_" + name, tag="acc_" + name) for name in names}
-        y = {name: keep.tile([P, G * (len(name) - 1)], F32, name="y_" + name) for name in names}
-        for g, name in enumerate("ab"):
-            for b in range(BLOCKS):
-                product(g, b, acc["%s%d" % (name, b)][:, 0:G])
-        for b in range(BLOCKS):
-            for h in range(2):
-                product(2 + h, b, acc["cd%d" % b][:, h * G : (h + 1) * G])
+        def bank(name):
+            return psum.tile([P, BANK], F32, name="acc_" + name, tag=name)
 
-        def drain_s(name):
-            nc.scalar.copy(out=y[name][:], in_=acc[name][:, 0 : G * (len(name) - 1)])
+        acc_a1, acc_a0, acc_b0, acc_b1 = bank("a1"), bank("a0"), bank("b0"), bank("b1")
+        acc_cd = [bank("cd%d" % b) for b in range(BLOCKS)]
+        product(0, 1, acc_a1[:, 0:G])
+        product(0, 0, acc_a0[:, 0:G])
+        product(1, 0, acc_b0[:, 0:G])
+        product(1, 1, acc_b1[:, 0:G])
+        for h in range(2):
+            for b in range(BLOCKS):
+                product(2 + h, b, acc_cd[b][:, h * G : (h + 1) * G])
 
         def places(d, v0, n):
             return to_sb[d][:, v0 // COLUMN : (v0 + n) // COLUMN]
@@ -136,25 +131,29 @@ def tile_picked_spconv_none_e_kernel(tc, xT, w1_words, w1_scales, w2_words, w2_s
         def scatter_s(d, b, v0, n, values):
             nc.scalar.activation(windows[d][b][:].indirect(places(d, v0, n)), values, COPY)
 
-        def drain_v(name):
-            nc.vector.tensor_copy(y[name][:], acc[name][:, 0 : G * (len(name) - 1)])
-
-        drain_s("a0")
-        drain_s("a1")
-        drain_v("b0")
-        scatter_s(0, 0, 0, G, y["a0"][:])
-        scatter_v(0, 1, 0, G, y["a1"][:])
-        drain_s("b1")
-        scatter_s(0, 0, G, G, y["b0"][:])
-        drain_v("cd0")
-        drain_v("cd1")
-        scatter_s(0, 1, G, G, y["b1"][:])
-        scatter_v(1, 0, 0, V, y["cd0"][:])
-        scatter_s(1, 1, 0, V, y["cd1"][:])
+        y_a1 = keep.tile([P, G], F32, name="y_a1")
+        y_a0 = keep.tile([P, G], F32, name="y_a0")
+        y_b0 = keep.tile([P, G], F32, name="y_b0", tag="codes2", align_bytes=64)
+        y_b1 = keep.tile([P, G], F32, name="y_b1", tag="codes3", align_bytes=64)
+        y_cd = [keep.tile([P, V], F32, name="y_cd%d" % b) for b in range(BLOCKS)]
+        nc.scalar.copy(out=y_a1[:], in_=acc_a1[:, 0:G])
+        nc.scalar.copy(out=y_a0[:], in_=acc_a0[:, 0:G])
+        scatter_s(0, 1, 0, G, y_a1[:])
+        scatter_v(0, 0, 0, G, y_a0[:])
+        nc.scalar.copy(out=y_b0[:], in_=acc_b0[:, 0:G])
+        nc.scalar.copy(out=y_cd[0][:], in_=acc_cd[0][:, 0:V])
+        nc.vector.tensor_copy(y_cd[1][:], acc_cd[1][:, 0:V])
+        nc.scalar.copy(out=y_b1[:], in_=acc_b1[:, 0:G])
+        scatter_v(0, 0, G, G, y_b0[:])
+        scatter_s(1, 0, 0, V, y_cd[0][:])
+        scatter_v(1, 1, 0, V, y_cd[1][:])
+        scatter_s(0, 1, G, G, y_b1[:])
 
         upper = keep.tile([P, U], F32, name="upper")
-        nc.vector.tensor_tensor(upper[:], windows[0][0][:], windows[1][0][:], ADD)
-        nc.sync.dma_start(out=out[0:P, :], in_=upper[:])
+        for u0 in range(0, U, U // 2):
+            cols = slice(u0, u0 + U // 2)
+            nc.vector.tensor_tensor(upper[:, cols], windows[0][0][:, cols], windows[1][0][:, cols], ADD)
+            nc.sync.dma_start(out=out[0:P, cols], in_=upper[:, cols])
         lower = keep.tile([P, U], F32, name="lower")
         for u0, n in LAST_PARTS:
             cols = slice(u0, u0 + n)

@@ -41,11 +41,13 @@ def tile_picked_spconv_none_e_kernel(tc, xT, w1_words, w1_scales, w2_words, w2_s
 
         def load_scales(d, scales, queue):
             for q in range(4):
-                rows = scales[0, 4 * q : 4 * q + 4, :].bitcast(I32)
                 queue.dma_start(
-                    out=w_scales[d][32 * q : 32 * q + 32, :].bitcast(I32),
-                    in_=rows.unsqueeze(0).broadcast_to([8, 4, N // 4]),
+                    out=w_scales[d][32 * q : 32 * q + 4, :].bitcast(I32),
+                    in_=scales[0, 4 * q : 4 * q + 4, :].bitcast(I32),
                 )
+
+        for d in range(TAPS):
+            nc.vector.memset(w_scales[d][:].bitcast(I32), 0)
 
         def load_words(d, words):
             nc.sync.dma_start(out=w_words[d][:].bitcast(I32), in_=words[0].rearrange("p n t -> p (n t)").bitcast(I32))
@@ -100,11 +102,11 @@ def tile_picked_spconv_none_e_kernel(tc, xT, w1_words, w1_scales, w2_words, w2_s
             )
 
         quantize(0)
-        nc.scalar.copy(
-            out=woven[1][:].rearrange("p v j -> p (v j)").bitcast(U32).rearrange("p (v u) -> p v u", u=2),
-            in_=pairs[:].rearrange("p u v e -> p (u v e)").bitcast(U32).rearrange("p (u v) -> p v u", u=2),
+        nc.scalar.copy(out=woven[2][:], in_=rows[0][:].rearrange("p j v -> p v j"))
+        nc.vector.tensor_copy(
+            woven[1][:].rearrange("p v j -> p (v j)").bitcast(I32).rearrange("p (v u) -> p v u", u=2),
+            pairs[:].rearrange("p u v e -> p (u v e)").bitcast(I32).rearrange("p (u v) -> p v u", u=2),
         )
-        weave_rows(2)
         weave_rows(3)
         for g in (1, 2, 3):
             quantize(g)

@@ -23,7 +23,8 @@ COLUMN = 16
 BANK = 512
 G = 128
 
-LAST_PARTS = ((0, 128), (128, 192), (320, 192))
+UPPER_PARTS = ((0, 256), (256, 256))
+LAST_PARTS = ((0, 256), (256, 256))
 
 
 def tile_picked_spconv_none_e_kernel(tc, xT, w1_words, w1_scales, w2_words, w2_scales, offs, to1, to2, out):
@@ -83,7 +84,9 @@ def tile_picked_spconv_none_e_kernel(tc, xT, w1_words, w1_scales, w2_words, w2_s
                 nc.scalar.activation(rows[g][:, j, :], planes[j][:].indirect(entries(V + g * G, G)), COPY)
 
         def weave_rows(g):
-            nc.vector.tensor_copy(woven[g][:], rows[g - 2][:].rearrange("p j v -> p v j"))
+            nc.vector.tensor_copy(
+                woven[g][:].rearrange("p (c i) j -> p c j i", i=4), rows[g - 2][:].rearrange("p j (c i) -> p c j i", i=4)
+            )
 
         def quantize(g):
             nc.vector.quantize_mx(out=codes[g][:].bitcast(FP8X4), scales=scales[g][:], in_=woven[g][:].rearrange("p v j -> p (v j)"))
@@ -102,7 +105,9 @@ def tile_picked_spconv_none_e_kernel(tc, xT, w1_words, w1_scales, w2_words, w2_s
             )
 
         quantize(0)
-        nc.scalar.copy(out=woven[2][:], in_=rows[0][:].rearrange("p j v -> p v j"))
+        nc.scalar.copy(
+            out=woven[2][:].rearrange("p (c i) j -> p c j i", i=4), in_=rows[0][:].rearrange("p j (c i) -> p c j i", i=4)
+        )
         nc.vector.tensor_copy(
             woven[1][:].rearrange("p v j -> p (v j)").bitcast(I32).rearrange("p (v u) -> p v u", u=2),
             pairs[:].rearrange("p u v e -> p (u v e)").bitcast(I32).rearrange("p (u v) -> p v u", u=2),
@@ -152,8 +157,8 @@ def tile_picked_spconv_none_e_kernel(tc, xT, w1_words, w1_scales, w2_words, w2_s
         scatter_s(0, 1, G, G, y_b1[:])
 
         upper = keep.tile([P, U], F32, name="upper")
-        for u0 in range(0, U, U // 2):
-            cols = slice(u0, u0 + U // 2)
+        for u0, n in UPPER_PARTS:
+            cols = slice(u0, u0 + n)
             nc.vector.tensor_tensor(upper[:, cols], windows[0][0][:, cols], windows[1][0][:, cols], ADD)
             nc.sync.dma_start(out=out[0:P, cols], in_=upper[:, cols])
         lower = keep.tile([P, U], F32, name="lower")

@@ -35,7 +35,8 @@ def tile_picked_spconv_none_e_kernel(tc, xT, w1_words, w1_scales, w2_words, w2_s
 
         offs_sb = keep.tile([P, TAPS * V // COLUMN], U16, name="offs_sb")
         to_sb = [keep.tile([P, V // COLUMN], U16, name="to%d" % d) for d in range(TAPS)]
-        planes = [keep.tile([P, T], F32, name="plane%d" % j) for j in range(PACK)]
+        front = keep.tile([P, 2 * T], F32, name="front")
+        planes = [front[:, 0:T], front[:, T : 2 * T]] + [keep.tile([P, T], F32, name="plane%d" % j)[:] for j in (2, 3)]
         w_words = [keep.tile([P, N], U32, name="w_words%d" % d, align_bytes=64) for d in range(TAPS)]
         w_scales = [keep.tile([P, N], U8, name="w_scales%d" % d, align_bytes=64) for d in range(TAPS)]
         x_rows = xT.rearrange("(p j) t -> j p t", j=PACK)
@@ -53,11 +54,11 @@ def tile_picked_spconv_none_e_kernel(tc, xT, w1_words, w1_scales, w2_words, w2_s
         def load_words(d, words):
             nc.sync.dma_start(out=w_words[d][:].bitcast(I32), in_=words[0].rearrange("p n t -> p (n t)").bitcast(I32))
 
-        nc.sync.dma_start(out=planes[0][:], in_=x_rows[0])
+        nc.sync.dma_start(out=front[:], in_=xT.rearrange("(p j) t -> p (j t)", j=PACK)[:, 0 : 2 * T])
         nc.sync.dma_start(offs_sb[:], offs)
         load_scales(0, w1_scales, nc.sync)
-        for j in (1, 2, 3):
-            nc.sync.dma_start(out=planes[j][:], in_=x_rows[j])
+        for j in (2, 3):
+            nc.sync.dma_start(out=planes[j], in_=x_rows[j])
         nc.sync.dma_start(to_sb[0][:], to1)
         load_words(0, w1_words)
         load_words(1, w2_words)
@@ -76,12 +77,12 @@ def tile_picked_spconv_none_e_kernel(tc, xT, w1_words, w1_scales, w2_words, w2_s
         codes = [keep.tile([P, G], U32, name="codes%d" % g, tag="codes%d" % g, align_bytes=64) for g in range(4)]
         scales = [keep.tile([P, G], U8, name="scales%d" % g, align_bytes=64) for g in range(4)]
         pairs = keep.tile([P, 2, G, 2], BF16, name="pairs")
-        rows = [keep.tile([P, PACK, G], BF16, name="rows%d" % g) for g in range(2)]
+        rows = [keep.tile([P, PACK, G], F32, name="rows%d" % g) for g in range(2)]
         for j in range(PACK):
-            nc.vector.tensor_copy(woven[0][:, :, j], planes[j][:].indirect(entries(0, G)))
-            nc.vector.tensor_copy(pairs[:, j // 2, :, j % 2], planes[j][:].indirect(entries(G, G)))
+            nc.vector.tensor_copy(woven[0][:, :, j], planes[j].indirect(entries(0, G)))
+            nc.vector.tensor_copy(pairs[:, j // 2, :, j % 2], planes[j].indirect(entries(G, G)))
             for g in range(2):
-                nc.scalar.activation(rows[g][:, j, :], planes[j][:].indirect(entries(V + g * G, G)), COPY)
+                nc.scalar.activation(rows[g][:, j, :], planes[j].indirect(entries(V + g * G, G)), COPY)
 
         def weave_rows(g):
             nc.vector.tensor_copy(

@@ -18,13 +18,13 @@ COPY = mybir.ActivationFunctionType.Copy
 P = 128
 PACK = 4
 TAPS = 2
-BLOCKS = N // P
+BANDS = N // P
 COLUMN = 16
 BANK = 512
 G = 128
-
-UPPER_PARTS = ((0, 256), (256, 256))
-LAST_PARTS = ((0, 256), (256, 256))
+PERIOD = 14
+TURNS = 5
+PART = 256
 
 
 def tile_picked_spconv_none_e_kernel(tc, xT, w1_words, w1_scales, w2_words, w2_scales, offs, to1, to2, out):
@@ -41,32 +41,33 @@ def tile_picked_spconv_none_e_kernel(tc, xT, w1_words, w1_scales, w2_words, w2_s
         w_scales = [keep.tile([P, N], U8, name="w_scales%d" % d, align_bytes=64) for d in range(TAPS)]
         x_rows = xT.rearrange("(p j) t -> j p t", j=PACK)
 
-        def load_scales(d, scales, queue):
-            for q in range(4):
-                queue.dma_start(
-                    out=w_scales[d][32 * q : 32 * q + 4, :].bitcast(I32),
-                    in_=scales[0, 4 * q : 4 * q + 4, :].bitcast(I32),
-                )
-
         for d in range(TAPS):
             nc.vector.memset(w_scales[d][:].bitcast(I32), 0)
+
+        def load_scales(d, scales):
+            rows = scales.bitcast(I32)
+            nc.sync.dma_start(
+                out=w_scales[d][0 : TURNS * PERIOD, :].bitcast(I32),
+                in_=rows[:, 0:PERIOD, :].to_broadcast([TURNS, PERIOD, N // 4]),
+            )
+            nc.sync.dma_start(out=w_scales[d][96:100, :].bitcast(I32), in_=rows[0, 12:16, :])
 
         def load_words(d, words):
             nc.sync.dma_start(out=w_words[d][:].bitcast(I32), in_=words[0].rearrange("p n t -> p (n t)").bitcast(I32))
 
         nc.sync.dma_start(out=front[:], in_=xT.rearrange("(p j) t -> p (j t)", j=PACK)[:, 0 : 2 * T])
         nc.sync.dma_start(offs_sb[:], offs)
-        load_scales(0, w1_scales, nc.sync)
         for j in (2, 3):
             nc.sync.dma_start(out=planes[j], in_=x_rows[j])
-        nc.sync.dma_start(to_sb[0][:], to1)
+        load_scales(0, w1_scales)
         load_words(0, w1_words)
+        nc.sync.dma_start(to_sb[0][:], to1)
+        load_scales(1, w2_scales)
         load_words(1, w2_words)
-        load_scales(1, w2_scales, nc.sync)
         nc.sync.dma_start(to_sb[1][:], to2)
 
-        windows = [[keep.tile([P, U], F32, name="window%d_%d" % (d, b)) for b in range(BLOCKS)] for d in range(TAPS)]
-        for b in range(BLOCKS):
+        windows = [[keep.tile([P, U], F32, name="window%d_%d" % (d, b)) for b in range(BANDS)] for d in range(TAPS)]
+        for b in range(BANDS):
             nc.vector.memset(windows[0][b][:], 0.0)
             nc.scalar.activation(windows[1][b][:], windows[0][b][:], COPY)
 
@@ -84,10 +85,8 @@ def tile_picked_spconv_none_e_kernel(tc, xT, w1_words, w1_scales, w2_words, w2_s
             for g in range(2):
                 nc.scalar.activation(rows[g][:, j, :], planes[j].indirect(entries(V + g * G, G)), COPY)
 
-        def weave_rows(g):
-            nc.vector.tensor_copy(
-                woven[g][:].rearrange("p (c i) j -> p c j i", i=4), rows[g - 2][:].rearrange("p j (c i) -> p c j i", i=4)
-            )
+        def runs(g):
+            return woven[g][:].rearrange("p (c i) j -> p c j i", i=4), rows[g - 2][:].rearrange("p j (c i) -> p c j i", i=4)
 
         def quantize(g):
             nc.vector.quantize_mx(out=codes[g][:].bitcast(FP8X4), scales=scales[g][:], in_=woven[g][:].rearrange("p v j -> p (v j)"))
@@ -106,28 +105,26 @@ def tile_picked_spconv_none_e_kernel(tc, xT, w1_words, w1_scales, w2_words, w2_s
             )
 
         quantize(0)
-        nc.scalar.copy(
-            out=woven[2][:].rearrange("p (c i) j -> p c j i", i=4), in_=rows[0][:].rearrange("p j (c i) -> p c j i", i=4)
-        )
+        nc.scalar.copy(*runs(2))
         nc.vector.tensor_copy(
             woven[1][:].rearrange("p v j -> p (v j)").bitcast(I32).rearrange("p (v u) -> p v u", u=2),
             pairs[:].rearrange("p u v e -> p (u v e)").bitcast(I32).rearrange("p (u v) -> p v u", u=2),
         )
-        weave_rows(3)
+        nc.vector.tensor_copy(*runs(3))
         for g in (1, 2, 3):
             quantize(g)
 
         def bank(name):
             return psum.tile([P, BANK], F32, name="acc_" + name, tag=name)
 
-        acc_a1, acc_a0, acc_b0, acc_b1 = bank("a1"), bank("a0"), bank("b0"), bank("b1")
-        acc_cd = [bank("cd%d" % b) for b in range(BLOCKS)]
-        product(0, 1, acc_a1[:, 0:G])
+        acc_a0, acc_a1, acc_b0, acc_b1 = bank("a0"), bank("a1"), bank("b0"), bank("b1")
+        acc_cd = [bank("cd%d" % b) for b in range(BANDS)]
         product(0, 0, acc_a0[:, 0:G])
+        product(0, 1, acc_a1[:, 0:G])
         product(1, 0, acc_b0[:, 0:G])
         product(1, 1, acc_b1[:, 0:G])
         for h in range(2):
-            for b in range(BLOCKS):
+            for b in range(BANDS):
                 product(2 + h, b, acc_cd[b][:, h * G : (h + 1) * G])
 
         def places(d, v0, n):
@@ -139,15 +136,15 @@ def tile_picked_spconv_none_e_kernel(tc, xT, w1_words, w1_scales, w2_words, w2_s
         def scatter_s(d, b, v0, n, values):
             nc.scalar.activation(windows[d][b][:].indirect(places(d, v0, n)), values, COPY)
 
-        y_a1 = keep.tile([P, G], F32, name="y_a1")
         y_a0 = keep.tile([P, G], F32, name="y_a0")
+        y_a1 = keep.tile([P, G], F32, name="y_a1")
         y_b0 = keep.tile([P, G], F32, name="y_b0", tag="codes2", align_bytes=64)
         y_b1 = keep.tile([P, G], F32, name="y_b1", tag="codes3", align_bytes=64)
-        y_cd = [keep.tile([P, V], F32, name="y_cd%d" % b) for b in range(BLOCKS)]
-        nc.scalar.copy(out=y_a1[:], in_=acc_a1[:, 0:G])
+        y_cd = [keep.tile([P, V], F32, name="y_cd%d" % b) for b in range(BANDS)]
         nc.scalar.copy(out=y_a0[:], in_=acc_a0[:, 0:G])
-        scatter_s(0, 1, 0, G, y_a1[:])
+        nc.scalar.copy(out=y_a1[:], in_=acc_a1[:, 0:G])
         scatter_v(0, 0, 0, G, y_a0[:])
+        scatter_s(0, 1, 0, G, y_a1[:])
         nc.scalar.copy(out=y_b0[:], in_=acc_b0[:, 0:G])
         nc.scalar.copy(out=y_cd[0][:], in_=acc_cd[0][:, 0:V])
         nc.vector.tensor_copy(y_cd[1][:], acc_cd[1][:, 0:V])
@@ -157,13 +154,9 @@ def tile_picked_spconv_none_e_kernel(tc, xT, w1_words, w1_scales, w2_words, w2_s
         scatter_v(1, 1, 0, V, y_cd[1][:])
         scatter_s(0, 1, G, G, y_b1[:])
 
-        upper = keep.tile([P, U], F32, name="upper")
-        for u0, n in UPPER_PARTS:
-            cols = slice(u0, u0 + n)
-            nc.vector.tensor_tensor(upper[:, cols], windows[0][0][:, cols], windows[1][0][:, cols], ADD)
-            nc.sync.dma_start(out=out[0:P, cols], in_=upper[:, cols])
-        lower = keep.tile([P, U], F32, name="lower")
-        for u0, n in LAST_PARTS:
-            cols = slice(u0, u0 + n)
-            nc.vector.tensor_tensor(lower[:, cols], windows[0][1][:, cols], windows[1][1][:, cols], ADD)
-            nc.sync.dma_start(out=out[P : 2 * P, cols], in_=lower[:, cols])
+        for b in range(BANDS):
+            total = keep.tile([P, U], F32, name="total%d" % b)
+            for u0 in range(0, U, PART):
+                cols = slice(u0, u0 + PART)
+                nc.vector.tensor_tensor(total[:, cols], windows[0][b][:, cols], windows[1][b][:, cols], ADD)
+                nc.sync.dma_start(out=out[b * P : (b + 1) * P, cols], in_=total[:, cols])

@@ -119,8 +119,8 @@ def tile_picked_spconv_none_e_kernel(tc, xT, w1_words, w1_scales, w2_words, w2_s
 
         acc_a0, acc_a1, acc_b0, acc_b1 = bank("a0"), bank("a1"), bank("b0"), bank("b1")
         acc_cd = [bank("cd%d" % b) for b in range(BANDS)]
-        product(0, 0, acc_a0[:, 0:G])
         product(0, 1, acc_a1[:, 0:G])
+        product(0, 0, acc_a0[:, 0:G])
         product(1, 0, acc_b0[:, 0:G])
         product(1, 1, acc_b1[:, 0:G])
         for h in range(2):
@@ -141,10 +141,10 @@ def tile_picked_spconv_none_e_kernel(tc, xT, w1_words, w1_scales, w2_words, w2_s
         y_b0 = keep.tile([P, G], F32, name="y_b0", tag="codes2", align_bytes=64)
         y_b1 = keep.tile([P, G], F32, name="y_b1", tag="codes3", align_bytes=64)
         y_cd = [keep.tile([P, V], F32, name="y_cd%d" % b) for b in range(BANDS)]
-        nc.scalar.copy(out=y_a0[:], in_=acc_a0[:, 0:G])
         nc.scalar.copy(out=y_a1[:], in_=acc_a1[:, 0:G])
-        scatter_v(0, 0, 0, G, y_a0[:])
+        nc.scalar.copy(out=y_a0[:], in_=acc_a0[:, 0:G])
         scatter_s(0, 1, 0, G, y_a1[:])
+        scatter_v(0, 0, 0, G, y_a0[:])
         nc.scalar.copy(out=y_b0[:], in_=acc_b0[:, 0:G])
         nc.scalar.copy(out=y_cd[0][:], in_=acc_cd[0][:, 0:V])
         nc.vector.tensor_copy(y_cd[1][:], acc_cd[1][:, 0:V])

from contextlib import ExitStack

import concourse.mybir as mybir

K, T, V, N, U = 512, 1024, 256, 256, 512
FLOPS = 2 * 2 * K * V * N

F32 = mybir.dt.float32
BF16 = mybir.dt.bfloat16
I32 = mybir.dt.int32
U32 = mybir.dt.uint32
U16 = mybir.dt.uint16
U8 = mybir.dt.uint8
FP8X4 = mybir.dt.float8_e4m3fn_x4
ADD = mybir.AluOpType.add
COPY = mybir.ActivationFunctionType.Copy

P = 128
PACK = 4
TAPS = 2
BANDS = N // P
COLUMN = 16
BANK = 512
G = 128
PERIOD = 14
TURNS = 5
PART = 256


def tile_picked_spconv_none_e_kernel(tc, xT, w1_words, w1_scales, w2_words, w2_scales, offs, to1, to2, out):
    nc = tc.nc
    with ExitStack() as ctx:
        keep = ctx.enter_context(tc.tile_pool(name="keep", bufs=1))
        psum = ctx.enter_context(tc.psum_pool(name="psum", bufs=1))

        offs_sb = keep.tile([P, TAPS * V // COLUMN], U16, name="offs_sb")
        to_sb = [keep.tile([P, V // COLUMN], U16, name="to%d" % d) for d in range(TAPS)]
        front = keep.tile([P, 2 * T], F32, name="front")
        planes = [front[:, 0:T], front[:, T : 2 * T]] + [keep.tile([P, T], F32, name="plane%d" % j)[:] for j in (2, 3)]
        w_words = [keep.tile([P, N], U32, name="w_words%d" % d, align_bytes=64) for d in range(TAPS)]
        w_scales = [keep.tile([P, N], U8, name="w_scales%d" % d, align_bytes=64) for d in range(TAPS)]
        x_rows = xT.rearrange("(p j) t -> j p t", j=PACK)

        for d in range(TAPS):
            nc.vector.memset(w_scales[d][:].bitcast(I32), 0)

        def load_scales(d, scales):
            rows = scales.bitcast(I32)
            nc.sync.dma_start(
                out=w_scales[d][0 : TURNS * PERIOD, :].bitcast(I32),
                in_=rows[:, 0:PERIOD, :].to_broadcast([TURNS, PERIOD, N // 4]),
            )
            nc.sync.dma_start(out=w_scales[d][96:100, :].bitcast(I32), in_=rows[0, 12:16, :])

        def load_words(d, words):
            nc.sync.dma_start(out=w_words[d][:].bitcast(I32), in_=words[0].rearrange("p n t -> p (n t)").bitcast(I32))

        nc.sync.dma_start(out=front[:], in_=xT.rearrange("(p j) t -> p (j t)", j=PACK)[:, 0 : 2 * T])
        nc.sync.dma_start(offs_sb[:], offs)
        for j in (2, 3):
            nc.sync.dma_start(out=planes[j], in_=x_rows[j])
        load_scales(0, w1_scales)
        load_words(0, w1_words)
        nc.sync.dma_start(to_sb[0][:], to1)
        load_scales(1, w2_scales)
        load_words(1, w2_words)
        nc.sync.dma_start(to_sb[1][:], to2)

        windows = [[keep.tile([P, U], F32, name="window%d_%d" % (d, b)) for b in range(BANDS)] for d in range(TAPS)]
        for b in range(BANDS):
            nc.vector.memset(windows[0][b][:], 0.0)
            nc.scalar.activation(windows[1][b][:], windows[0][b][:], COPY)

        def entries(first, n):
            return offs_sb[:, first // COLUMN : (first + n) // COLUMN]

        woven = [keep.tile([P, G, PACK], BF16, name="woven%d" % g, align_bytes=64) for g in range(4)]
        codes = [keep.tile([P, G], U32, name="codes%d" % g, tag="codes%d" % g, align_bytes=64) for g in range(4)]
        scales = [keep.tile([P, G], U8, name="scales%d" % g, align_bytes=64) for g in range(4)]
        pairs = keep.tile([P, 2, G, 2], BF16, name="pairs")
        rows = [keep.tile([P, PACK, G], F32, name="rows%d" % g) for g in range(2)]
        for j in range(PACK):
            nc.vector.tensor_copy(woven[0][:, :, j], planes[j].indirect(entries(0, G)))
            nc.vector.tensor_copy(pairs[:, j // 2, :, j % 2], planes[j].indirect(entries(G, G)))
            for g in range(2):
                nc.scalar.activation(rows[g][:, j, :], planes[j].indirect(entries(V + g * G, G)), COPY)

        def runs(g):
            return woven[g][:].rearrange("p (c i) j -> p c j i", i=4), rows[g - 2][:].rearrange("p j (c i) -> p c j i", i=4)

        def quantize(g):
            nc.vector.quantize_mx(out=codes[g][:].bitcast(FP8X4), scales=scales[g][:], in_=woven[g][:].rearrange("p v j -> p (v j)"))

        def product(g, b, acc):
            d = g // 2
            m = slice(b * P, (b + 1) * P)
            nc.tensor.matmul_mx(
                out=acc,
                lhsT=w_words[d][:, m].bitcast(FP8X4),
                lhsT_scale=w_scales[d][:, m],
                rhs=codes[g][:].bitcast(FP8X4),
                rhs_scale=scales[g][:],
                start=True,
                stop=True,
            )

        quantize(0)
        nc.scalar.copy(*runs(2))
        nc.vector.tensor_copy(
            woven[1][:].rearrange("p v j -> p (v j)").bitcast(I32).rearrange("p (v u) -> p v u", u=2),
            pairs[:].rearrange("p u v e -> p (u v e)").bitcast(I32).rearrange("p (u v) -> p v u", u=2),
        )
        nc.vector.tensor_copy(*runs(3))
        for g in (1, 2, 3):
            quantize(g)

        def bank(name):
            return psum.tile([P, BANK], F32, name="acc_" + name, tag=name)

        acc_a0, acc_a1, acc_b0, acc_b1 = bank("a0"), bank("a1"), bank("b0"), bank("b1")
        acc_cd = [bank("cd%d" % b) for b in range(BANDS)]
        product(0, 1, acc_a1[:, 0:G])
        product(0, 0, acc_a0[:, 0:G])
        product(1, 0, acc_b0[:, 0:G])
        product(1, 1, acc_b1[:, 0:G])
        for h in range(2):
            for b in range(BANDS):
                product(2 + h, b, acc_cd[b][:, h * G : (h + 1) * G])

        def places(d, v0, n):
            return to_sb[d][:, v0 // COLUMN : (v0 + n) // COLUMN]

        def scatter_v(d, b, v0, n, values):
            nc.vector.tensor_copy(windows[d][b][:].indirect(places(d, v0, n)), values)

        def scatter_s(d, b, v0, n, values):
            nc.scalar.activation(windows[d][b][:].indirect(places(d, v0, n)), values, COPY)

        y_a0 = keep.tile([P, G], F32, name="y_a0")
        y_a1 = keep.tile([P, G], F32, name="y_a1")
        y_b0 = keep.tile([P, G], F32, name="y_b0", tag="codes2", align_bytes=64)
        y_b1 = keep.tile([P, G], F32, name="y_b1", tag="codes3", align_bytes=64)
        y_cd = [keep.tile([P, V], F32, name="y_cd%d" % b) for b in range(BANDS)]
        nc.scalar.copy(out=y_a1[:], in_=acc_a1[:, 0:G])
        nc.scalar.copy(out=y_a0[:], in_=acc_a0[:, 0:G])
        scatter_s(0, 1, 0, G, y_a1[:])
        scatter_v(0, 0, 0, G, y_a0[:])
        nc.scalar.copy(out=y_b0[:], in_=acc_b0[:, 0:G])
        nc.scalar.copy(out=y_cd[0][:], in_=acc_cd[0][:, 0:V])
        nc.vector.tensor_copy(y_cd[1][:], acc_cd[1][:, 0:V])
        nc.scalar.copy(out=y_b1[:], in_=acc_b1[:, 0:G])
        scatter_v(0, 0, G, G, y_b0[:])
        scatter_s(1, 0, 0, V, y_cd[0][:])
        scatter_v(1, 1, 0, V, y_cd[1][:])
        scatter_s(0, 1, G, G, y_b1[:])

        for b in range(BANDS):
            total = keep.tile([P, U], F32, name="total%d" % b)
            for u0 in range(0, U, PART):
                cols = slice(u0, u0 + PART)
                nc.vector.tensor_tensor(total[:, cols], windows[0][b][:, cols], windows[1][b][:, cols], ADD)
                nc.sync.dma_start(out=out[b * P : (b + 1) * P, cols], in_=total[:, cols])
